import numpy as np, ml_dtypes
CORES = [1,5,17,21,33,37,49,53]
N = 8
BF = ml_dtypes.bfloat16
W, H0, L, RO, Q = 4096, 1536, 192, 3, 2
def base(rng):
    price = rng.integers(0, 101, (N, 8, 1, W)) + rng.integers(0, 28, (N, 8, 16, W))
    packs = rng.integers(0, W, (N, 8, 16, H0)); prev = rng.integers(0, H0, (N, 8, H0)); lots = rng.integers(0, W, (N, 8, 16, L))
    lots[:, :, 0, ::4] = lots[:1, :, 0, ::4]
    o = np.stack([rng.permutation(np.array([5, 20, 35, 50, 60, 70, 80, 90])) for q in range(N)])
    slack = o[:, :, None, None] + rng.integers(0, 9, (N, 8, 16, RO))
    return price, packs, prev, lots, rng.integers(1, 8, (N, 8, 16)), rng.integers(0, 16, (N, 8, 16)), slack
def pack(price, packs, prev, lots, inc, wt, slack):
    c = lambda a, n: np.ascontiguousarray(np.reshape(a, (N, 128, n))).astype(np.int32)
    return {"price": np.ascontiguousarray(price.reshape(N, 128, W)).astype(np.float32).astype(BF), "packs": c(packs, H0), "prev": np.ascontiguousarray(prev).astype(np.int32),
            "lots": c(lots, L), "inc": c(inc, 1), "wt": c(wt, 1), "slack": c(slack, RO)}
def edge(rng, hi, *s):
    return np.where(rng.random(s) < 0.2, rng.integers(0, hi + 1, s), hi * rng.integers(0, 2, s))
def setup_inputs(rng):
    return pack(*base(rng))
def setup_inputs_spread(rng):
    price, packs, prev, lots, inc, wt, slack = base(rng)
    price = np.minimum((np.exp2(7.65 * rng.random((N, 8, 1, W))) * rng.random((N, 8, 16, W))).astype(np.int64), 200)
    packs = np.minimum((W * rng.random((N, 8, 16, H0)) ** 3).astype(np.int64), W - 1)
    lots = W - 1 - np.minimum((W * rng.random((N, 8, 16, L)) ** 2).astype(np.int64), W - 1)
    prev = np.minimum((H0 * rng.random((N, 8, H0)) ** 2).astype(np.int64), H0 - 1)
    slack = np.minimum(np.exp2(8 * rng.random((N, 8, 1, 1)) * rng.random((N, 8, 16, RO))).astype(np.int64) - 1, 255)
    return pack(price, packs, prev, lots, inc, wt, slack)
def setup_inputs_ends(rng):
    hi = np.where(np.arange(8) == 6, 127, 200)[None, :, None, None]
    k = rng.integers(0, 3, (N, 8, 1, W)); price = hi * np.where(k == 2, rng.integers(0, 2, (N, 8, 16, W)), k)
    price[..., 0] = 0; price[..., W - 1] = hi[..., 0]
    price[:, 2:4, :, 0] = 200; price[:, 2:4, :, W - 1] = 0; price[:, 5, 9:, W - 1] = 0
    packs = edge(rng, W - 1, N, 8, 16, H0); prev = edge(rng, H0 - 1, N, 8, H0); lots = edge(rng, W - 1, N, 8, 16, L)
    inc = 1 + 6 * rng.integers(0, 2, (N, 8, 16)); inc[:, 7] = 7; inc[:, 6, 0] = 1
    o = np.argsort(rng.random((N, 8, 16)), axis=2)
    slack = np.repeat((255 * (o >= np.array([16, 9, 16, 9, 12, 16, 8, 8])[None, :, None]))[..., None], RO, axis=3)
    wt = 15 * rng.integers(0, 2, (N, 8, 16)); wt[:, 7] = 0
    full = np.array([15] * 8 + [9] + [0] * 7); wt[:, 6] = full[o[:, 6]]; wt[:, 0] = full[o[:, 0]]
    c = np.array([0, 3, L - 1]); lots[:, 6, 0, c] = W - 1; lots[:, 6, 15, c] = W - 1
    v = np.arange(W)
    back = lambda t, to: int(np.argmax(((v + (v >> 5) + 77 * (t + 1)) & (W - 1)) == to))
    lots[:, 7, 0, c] = W - 1; lots[:, 7, 1, c] = back(0, W - 1); lots[:, 7, 2, c] = back(0, back(1, W - 1))
    return pack(price, packs, prev, lots, inc, wt, slack)
def setup_inputs_corners(rng):
    price, packs, prev, lots, inc, wt, slack = base(rng); a = np.arange(H0)
    kinds = [a, np.maximum(a - 1, 0), 0 * a, 0 * a + H0 - 1, (a + 1) % H0, a ^ 1, H0 - L + a % L]
    for q in range(N):
        for g, k in enumerate(rng.permutation(8)):
            if k < 7: prev[q, g] = kinds[int(k)]
            wt[q, g] = (0, 15, 1, 7)[int(rng.integers(0, 4))] if k < 4 else wt[q, g]
            inc[q, g] = 1 if k % 3 == 0 else 7 if k % 3 == 1 else inc[q, g]
    s = [int(g) for g in rng.permutation(8)]
    for g in s[:4]: slack[:, g] = 255
    lots[:, s[0], :RO] = W - 1; wt[:, s[0]] = 0; price[:, s[0], :, W - 1] = 127; inc[:, s[0]] = 7
    lots[:, s[1], 0] = 0; price[:, s[1], :, 0] = 127 * rng.integers(0, 2, (N, 16))
    m = rng.permutation(W); lots[:, s[2], 0] = m[(np.arange(N * L) % (W - 1) + 1).reshape(N, L)]; lots[int(rng.integers(0, N)), s[2], 0, L - 1] = m[0]
    for q in range(N): lots[q, s[3], 0] = rng.permutation(W)[:L]
    packs[:, s[4], :, H0 - L:] = lots[:, s[4]]
    slack[:, s[4]] = 0; slack[:, s[5]] = 0; h = W // 2
    price[:, s[5], :, :h] = rng.integers(0, 3, (N, 16, h)); price[:, s[5], :, h:] = 127; lots[:, s[5]] = rng.integers(h, W, (N, 16, L)); packs[:, s[5]] = rng.integers(0, h, (N, 16, H0))
    nxt = lambda z, u, t: (((z * (2 * u + 1)) >> 5) + z + 77 * (t + 1)) & (W - 1)
    g = s[6]; b = int(rng.integers(0, N)); k = L // 2
    wt[:, g] = 0; inc[:, g] = 7; inc[b, g] = 1 + rng.permutation(16) % 5
    slack[:, g] = 255; slack[:, g, :, RO - 1] = 254 - rng.integers(0, 55, (N, 16)) * (np.arange(N) % 2)[:, None]
    e = rng.integers(0, W, L); own = nxt(e, 0, 0); own[k:] = nxt(own[k:], 0, 1)
    lots[:, g, 0] = own; lots[:, g, 1, :k] = e[:k]; lots[:, g, 2, k:] = e[k:]
    dear = np.zeros(W, bool); dear[own] = True; low = rng.random(W) < 0.5
    v = 200 - (rng.random((N, 16, W)) * np.where(low, 32, 8)).astype(np.int64)
    v[b] = np.where(low, rng.integers(0, 4, (16, W)), v[b])
    price[:, g] = np.where(dear, v, rng.integers(0, 3, W))
    g = s[7]; wt[:, g] = 15; inc[:, g] = 7; slack[:, g] = 255; price[:, g] = 200
    e = rng.integers(0, W, L); lots[:, g, 1] = e; lots[:, g, 0] = nxt(e, (16 * 15 * 200) & 1023, 0)
    return pack(price, packs, prev, lots, inc, wt, slack)
def setup_inputs_ties(rng):
    price, packs, prev, lots, inc, wt, slack = base(rng)
    s0 = rng.integers(0, 21, (N, 8, 16)); b = rng.integers(0, 106, (N, 8, 16)); slack = np.repeat(s0[..., None], RO, axis=3)
    n = rng.choice(np.array([0, 7, 8, 9, 10, 16]), (N, 8, 1, W)); low = rng.random((N, 8, 1, W)) < 0.5
    o = np.argsort(rng.random((N, 8, W, 16)), axis=3).transpose(0, 1, 3, 2)
    price = b[..., None] + np.where(low, 0, s0[..., None] + (o < n))
    return pack(price, packs, prev, lots, inc, wt, slack)
def check_inputs(d):
    bad = []
    for k, lo, hi in (("price", 0, 200), ("packs", 0, W - 1), ("prev", 0, H0 - 1), ("lots", 0, W - 1), ("inc", 1, 7), ("wt", 0, 15), ("slack", 0, 255)):
        v = np.asarray(d[k]).astype(np.float64)
        if not (np.min(v) >= lo and np.max(v) <= hi): bad.append("range of " + k)
        elif np.any(v != np.floor(v)): bad.append("whole numbers in " + k)
    return bad
def pick(p, t):
    return np.take_along_axis(p, t.reshape(N, 8, 1, 16 * L), 3).reshape(N, 8, 16, 16, L)
def reference(price, packs, prev, lots, inc, wt, slack):
    p = price.astype(np.float32).astype(np.int64).reshape(N, 8, 16, W)
    h = np.zeros((N, 8, 16, H0 + RO * L), np.int64); h[..., :H0] = packs.reshape(N, 8, 16, H0)
    v = np.zeros((N, 8, H0 + RO * L), np.int64); v[..., :H0] = prev
    t = lots.astype(np.int64).reshape(N, 8, 16, L)
    up = inc.astype(np.int64).reshape(N, 8, 16, 1); wr = wt.astype(np.int64).reshape(N, 8, 16, 1); sl = slack.astype(np.int64).reshape(N, 8, 16, RO)
    a = np.zeros((N, 8, L), np.int64) + (H0 - L + np.arange(L))
    for rnd in range(RO):
        x = pick(p, t); bind = np.zeros((N, 8, L), np.int64) - 1
        for e in range(Q):
            anc = np.take_along_axis(h, a[:, :, None, :], 3); y = pick(p, anc)
            rows = np.add.reduce((x - y > sl[:, :, :, rnd][:, :, :, None, None]).astype(np.int64), axis=2)
            rev = rows >= 9
            t = np.where(rev, anc, t); x = np.where(rev[:, :, None], y, x)
            bind = np.where(np.any(rev, axis=2), a, bind); last = a
            a = np.take_along_axis(v, a, 2)
        lo = H0 + L * rnd
        h[..., lo:lo + L] = t; v[..., lo:lo + L] = np.where(bind >= 0, bind, last)
        flag = np.zeros((N, 8, W), np.int64); np.put_along_axis(flag, t[:, :, rnd], 1, 2)
        offer = p * flag[:, :, None]; s = np.add.reduce(offer, axis=0)[None] - offer
        if rnd + 1 < RO:
            u = np.add.reduce(wr * np.max(x, axis=3), axis=2) & 1023
            t = (((t * (2 * u + 1)[:, :, None]) >> 5) + t + 77 * (rnd + 1)) & (W - 1)
            a = np.zeros((N, 8, L), np.int64) + (lo + np.arange(L))
        p = np.minimum(p + ((up * s) >> 6), 255)
    return {"yp": p.reshape(N, 128, W).astype(np.float32).astype(BF), "yh": np.ascontiguousarray(h[..., H0:]).reshape(N, 128, RO * L).astype(np.float32), "yv": np.ascontiguousarray(v[..., H0:]).astype(np.float32)}

@@ -1,0 +1,494 @@
+import numpy as np
+from concourse.bass import DstId, RemoteDMATransfer
+from concourse.mybir import dt, AluOpType, AxisListType, ActivationFunctionType
+
+A = AluOpType
+AF = ActivationFunctionType
+MAGIC = 12582912.0
+NL = 192
+E = 16 * NL
+W = 4096
+WW = W + 16
+CUTS = [0, 64, 128, 192]
+BLOCKS = [0, 1024, 2048, 3072, W]
+NB = len(BLOCKS) - 1
+SCRATCH = {}
+for _d, _n, _names in (
+        ("bfloat16", W, "ph c pl pf"), ("bfloat16", WW, "w0 w1 w2"), ("float32", WW, "u"), ("int32", 1536, "pk"),
+        ("int32", NL, "lt pnr ui uj pr ps sm tn"), ("int32", 12, "pvi"), ("uint16", 24, "pvo of"), ("uint16", 12, "vl"),
+        ("int32", 8, "cs cso pci"), ("float32", 8, "csf nsl cof pcf"), ("float32", 128, "cd"), ("float32", 384, "ts par12"),
+        ("bfloat16", 128, "bo nb eq idm qk dg qm wth wto cstb"), ("bfloat16", 512, "oneb"), ("bfloat16", 2048, "sel16"),
+        ("bfloat16", E, "rm ind x2 sc"), ("float32", E, "xs0 xs1"), ("bfloat16", NL, "mk0 mk1 cse v0"),
+        ("float32", NL, "cm dm onef pb0 pb1 pb2 a1f sel t1f t2f0 t2f1 t2f2 o2f par0 b1f tc cmk cs1 cs2"),
+        ("uint16", NL, "tu0 a0u a1u t1u t2u0 t2u1 t2u2 o2u b1u tnu"), ("float32", 12, "ct1 ct2"),
+        ("uint16", 576, "m4u mo"), ("float32", 576, "mof")):
+    for _k in _names.split():
+        SCRATCH[_k] = ("sbuf", [128, _n], _d)
+MSG = []
+for _k, _n, _d in [("cst", 1, "int32"), ("pri", 512, "bfloat16"), ("t2", 24, "uint16"), ("m4", 72, "uint16"), ("y1", 24, "float32"),
+                   ("y2", 24, "float32"), ("par", 3, "float32")] + [("o%d" % _b, (BLOCKS[_b + 1] - BLOCKS[_b]) // 8, "bfloat16") for _b in range(NB)]:
+    MSG.append(_k)
+    SCRATCH["s_" + _k] = SCRATCH["l_" + _k] = ("dram", [8, 128, _n], _d)
+BANKS = ["cn0", "cn1", "vs", "db0", "db1", "db2", "db3", "db4"]
+for _k in BANKS:
+    SCRATCH[_k] = ("psum", [128, 512], "float32")
+SEMAPHORES = ["vv", "ss", "pe", "gg", "lsem"] + ["d%d" % _i for _i in range(64)] + ["ar_" + _m for _m in MSG]
+
+
+def rank_program(g, core, T, topo):
+    rank = T.rank_of(core)
+    if rank is None:
+        return
+    cores = [int(c) for c in T.cores]
+    N = len(cores)
+
+    eng = {"v": g.vector, "s": g.scalar, "p": g.tensor, "g": g, "y": g.sync}
+    sem_of = {"v": "vv", "s": "ss", "p": "pe", "g": "gg"}
+    count = {"vv": 0, "ss": 0, "pe": 0, "gg": 0, "d": 0}
+    know = {q: {} for q in eng}
+    snap = {}
+    hist = {}
+    total = {}
+    seen = {}
+
+    def wait(q, sem, val):
+        if know[q].get(sem, 0) >= val:
+            return
+        eng[q].wait_ge(T.sem[sem], val)
+        seen[sem] = max(seen.get(sem, 0), val)
+        know[q][sem] = val
+        for k, n in snap.get((sem, val), {}).items():
+            know[q][k] = max(know[q].get(k, 0), n)
+
+    def settle(q, reads, writes, is_dma):
+        for (b, lo, hi), wr in [(r, False) for r in reads] + [(w, True) for w in writes]:
+            bank = b in BANKS
+            for e in hist.get(b, []):
+                over = e[0] < hi and lo < e[1]
+                if e[2] == q and not is_dma:
+                    need = over and e[5]
+                else:
+                    need = bank or (over and (wr or e[5]))
+                if need:
+                    wait(q, e[3], e[4])
+
+    def record(q, sem, val, reads, writes):
+        for (b, lo, hi) in writes:
+            hist[b] = [e for e in hist.get(b, []) if not (lo <= e[0] and e[1] <= hi)] + [(lo, hi, q, sem, val, True)]
+        for (b, lo, hi) in reads:
+            old = hist.get(b, [])
+            hist[b] = [e for e in old if not (e[:3] == (lo, hi, q) and not e[5] and q != "d")] + [(lo, hi, q, sem, val, False)]
+
+    def run(q, reads, writes, *fns):
+        settle(q, reads, writes, False)
+        for f in fns[:-1]:
+            f()
+        sem = sem_of[q]
+        count[sem] += 1
+        val = total[sem] = count[sem]
+        fns[-1]().then_inc(T.sem[sem], 1)
+        snap[(sem, val)] = dict(know[q])
+        snap[(sem, val)][sem] = val
+        record(q, sem, val, reads, writes)
+
+    def dma(q, out, in_, reads, writes):
+        settle(q, reads, writes, True)
+        sem = "d%d" % count["d"]
+        count["d"] += 1
+        total[sem] = 16
+        eng[q].dma_start(out, in_).then_inc(T.sem[sem], 16)
+        snap[(sem, 16)] = dict(know[q])
+        record("d", sem, 16, reads, writes)
+
+    def full(name):
+        return (name, 0, 1 << 20)
+
+    def col(x, lo=0, hi=NL):
+        b, o = (x, 0) if x in SCRATCH else x
+        return T[b][:, o + lo:o + hi], (b, o + lo, o + hi)
+
+    def V(reads, writes, f):
+        run("v", reads, writes, f)
+
+    def S(reads, writes, f):
+        run("s", reads, writes, f)
+
+    v, s, te = g.vector, g.scalar, g.tensor
+
+    def vt(out, in0, in1, op):
+        return lambda: v.tensor_tensor(out, in0, in1, op)
+
+    def vc(out, in_):
+        return lambda: v.tensor_copy(out, in_)
+
+    def v1(out, in0, s1, op):
+        return lambda: v.tensor_scalar(out, in0, s1, None, op)
+
+    def v2(out, in0, s1, s2, op0, op1):
+        return lambda: v.tensor_scalar(out, in0, s1, s2, op0, op1)
+
+    def fill(b, lo, hi, x):
+        V([], [(b, lo, hi)], lambda: v.memset(T[b][:, lo:hi], x))
+
+    others = [(rank + j) % N for j in range(1, N)]
+    away = [d for d in others if topo.chip(cores[d]) != topo.chip(core)]
+    near = [d for d in others if topo.chip(cores[d]) == topo.chip(core)]
+    offe = topo.engines(core, cores[away[0]])
+    one = [e for e in topo.engines(core, cores[near[0]]) if e not in offe]
+    turn = [0]
+    arrive = {m: 0 for m in MSG}
+
+    def fused(m, plan):
+        settle("g", [full("s_" + m)], [], True)
+        tr = []
+        for d, es in plan:
+            rid, pid, _e = topo.addr(cores[d])
+            tr.append(RemoteDMATransfer(dst_ids=[DstId(rid=rid, pnc=pid)], dma_engine_mask=sum(1 << e for e in es),
+                                        remote_sem=T.sem["ar_" + m], src=T["s_" + m][d], dst=T["l_" + m][rank]))
+        g.remote_dma_fused(tr, local_sem=T.sem.lsem)
+        n = sum(len(es) for d, es in plan)
+        total["lsem"] = total.get("lsem", 0) + n
+        arrive[m] += n
+
+    def send(m):
+        plan = [(d, [offe[(turn[0] + j) % len(offe)]]) for j, d in enumerate(away)]
+        turn[0] += len(away)
+        fused(m, plan + [(d, one[0:3:2]) for d in near])
+
+    def send_wide(m):
+        fused(m, [(d, offe[2 * j:2 * j + 2]) for j, d in enumerate(away[:4])] + [(d, one[0:3:2]) for d in near])
+        fused(m, [(d, offe[4 * j:4 * j + 4]) for j, d in enumerate(away[4:])])
+
+    def landed(q, m):
+        total["ar_" + m] = arrive[m]
+        wait(q, "ar_" + m, arrive[m])
+
+    def stage(m, in_, reads):
+        dma("y", T["s_" + m][:], in_, reads, [full("s_" + m)])
+
+    def own(m):
+        dma("y", T["l_" + m][rank], T["s_" + m][rank], [full("s_" + m)], [full("l_" + m)])
+
+    def take(q, m, out, writes):
+        landed(q, m)
+        dma(q, out, T["l_" + m][:], [full("l_" + m)], writes)
+
+    fill("cs", 0, 8, 0)
+    fill("pnr", 0, NL, 0)
+    dma("y", T.ph[:], T.price[:], [], [full("ph")])
+    dma("s", T.lt[:], T.lots[:], [], [full("lt")])
+    dma("s", T.cs[:, 0:3], T.slack[:], [], [("cs", 0, 3)])
+    dma("s", T.pk[:, 1344:1536], T.packs[:, 1344:1536], [], [("pk", 1344, 1536)])
+    dma("s", T.pvi[:], T.prev[:, 1344:1536], [], [full("pvi")])
+    dma("y", T.pk[:, 0:1344], T.packs[:, 0:1344], [], [("pk", 0, 1344)])
+    dma("s", T.cs[:, 3:4], T.inc[:], [], [("cs", 3, 4)])
+    dma("s", T.cs[:, 4:5], T.wt[:], [], [("cs", 4, 5)])
+    stage("pri", T.price[:], [])
+    dma("y", T.pnr[0:128:16, :], T.prev[:, 1344:1536], [], [full("pnr")])
+    stage("cst", T.cs[:], [full("cs")])
+    own("pri")
+    own("cst")
+
+    def iota(b, lo, hi, pat, base, cm, **kw):
+        run("g", [], [(b, lo, hi)], lambda: g.iota(T[b][:, lo:hi], pat, base, cm, **kw))
+    small = {"allow_small_or_imprecise_dtypes": True}
+    iota("pci", 0, 1, [[0, 1]], 0, 1)
+    iota("cd", 0, 128, [[1, 8], [0, 16]], 0, 0, **small)
+    iota("cm", 0, NL, [[0, 12], [1, 16]], 0, 0, **small)
+    for t in range(3):
+        iota("pb%d" % t, 0, NL, [[1, NL]], 1344 + NL * t, 0, **small)
+    V([("pci", 0, 1)], [("pci", 1, 2)], v1(T.pci[:, 1:2], T.pci[:, 0:1], 15, A.bitwise_and))
+    V([("pci", 0, 1)], [("pci", 2, 3)], v1(T.pci[:, 2:3], T.pci[:, 0:1], 4, A.logical_shift_right))
+    V([("pci", 1, 3)], [("pcf", 1, 3)], vc(T.pcf[:, 1:3], T.pci[:, 1:3]))
+    V([("pcf", 1, 2)], [("pcf", 3, 4)], v1(T.pcf[:, 3:4], T.pcf[:, 1:2], float(W), A.add))
+    for t in range(3):
+        V([("pcf", 1, 2)], [("pcf", 4 + t, 5 + t)], v1(T.pcf[:, 4 + t:5 + t], T.pcf[:, 1:2], float(t), A.is_equal))
+    V([full("cd"), ("pcf", 2, 3)], [full("bo")], v1(T.bo[:], T.cd[:], T.pcf[:, 2:3], A.is_equal))
+    fill("sel16", 0, 2048, 0.0)
+    V([full("lt")], [full("tu0")], vc(T.tu0[:], T.lt[:]))
+    V([full("cs")], [full("csf")], vc(T.csf[:], T.cs[:]))
+    V([full("csf")], [full("nsl")], v1(T.nsl[:], T.csf[:], -1.0, A.mult))
+    for k in range(16):
+        V([full("bo")], [("sel16", 128 * k, 128 * k + 128)], vc(T.sel16[:, 128 * k + k:128 * k + 128:16], T.bo[:, 0:128:16]))
+    V([("pk", 1344, 1536)], [full("a0u")], vc(T.a0u[:], T.pk[:, 1344:1536]))
+
+    def more_constants():
+        V([full("bo")], [full("nb")], v1(T.nb[:], T.bo[:], -17.0, A.mult))
+        fill("rm", 0, E, 1.0)
+        V([full("rm")], [full("rm")], lambda: v.memset(T.rm[:, 0:E:16], 0.0))
+        V([full("bo"), full("csf")], [full("wth")], v1(T.wth[:], T.bo[:], T.csf[:, 4:5], A.mult))
+        fill("w0", 0, WW, 0.0)
+
+    def second_package():
+        V([full("pvi")], [full("pvo")], vc(T.pvo[:, 0:24:2], T.pvi[:]))
+        for c in range(12):
+            V([full("pvo"), full("pk")], [("a1f", c, c + 1)], vc(T.a1f[:, c:NL:12], T.pk[:, 0:1536].indirect(T.pvo[:, 2 * c:2 * c + 1])))
+        V([full("a1f")], [full("a1u")], vc(T.a1u[:], T.a1f[:]))
+
+    def step1(tab, low, tu, tn, a0u, a0n, a1u, a1n, bias, t2f, t2u, filler):
+        def lanes(x, j):
+            return col(x, CUTS[j], CUTS[j + 1])
+
+        def items(b, j):
+            return col(b, 16 * CUTS[j], 16 * CUTS[j + 1])
+
+        def xg(tr, lst, j):
+            l, o = lanes(lst, j), items("xs%d" % tr, j)
+            S([full(tab), l[1], full(bias[0])], [o[1]],
+              lambda: s.activation(o[0], T[tab][:, 0:W].indirect(l[0]), AF.Identity, bias=T[bias[0]][:, bias[1]:bias[1] + 1]))
+
+        def compare(tr, lst, j):
+            l, x, o, n = lanes(lst, j), items("xs%d" % tr, j), items("ind", j), CUTS[j + 1] - CUTS[j]
+            V([full(tab), l[1], x[1]], [o[1]], vt(o[0], T[tab][:, 0:W].indirect(l[0]), x[0], A.is_lt if low else A.is_gt))
+            cn = "cn%d" % ((tr * 3 + j) % 2)
+            run("p", [o[1], full("sel16")], [(cn, 0, n)],
+                *[(lambda k=k: te.matmul(T[cn][:, 0:n], T.sel16[:, 128 * k:128 * k + 128], T.ind[:, o[1][1] + k:o[1][2]:16],
+                                         k == 0, k == 15)) for k in range(16)])
+
+        def choose(tr, cur, newf, newu, j):
+            n = CUTS[j + 1] - CUTS[j]
+            cn = "cn%d" % ((tr * 3 + j) % 2)
+            m, d, p = lanes("mk%d" % tr, j), lanes("vs", j), lanes(("vs", NL), j)
+            c, f, u = lanes(cur, j), lanes(newf, j), lanes(newu, j)
+            V([(cn, 0, n)], [m[1]], v1(m[0], T[cn][:, 0:n], 8.5, A.is_ge))
+            V([d[1], m[1]], [p[1]], vt(p[0], d[0], m[0], A.mult))
+            V([p[1], c[1]], [f[1]], vt(f[0], p[0], c[0], A.add))
+            V([f[1]], [u[1]], vc(u[0], f[0]))
+            if tr == 0:
+                a = lanes(a1n, j)
+                V([a[1], f[1]], [d[1]], vt(d[0], a[0], f[0], A.subtract))
+
+        def x2g(j):
+            l, o = lanes(t2u, j), items("x2", j)
+            kw = {} if low else {"scale": -1.0, "bias": 255.0}
+            S([full(tab), l[1]], [o[1]], lambda: s.activation(o[0], T[tab][:, 0:W].indirect(l[0]), AF.Identity, **kw))
+
+        for j in range(3):
+            xg(0, tu, j)
+        d, a, t = col("vs"), col(a0n), col(tn)
+        V([a[1], t[1]], [d[1]], vt(d[0], a[0], t[0], A.subtract))
+        filler[0]()
+        compare(0, a0u, 0)
+        filler[1]()
+        compare(0, a0u, 1)
+        choose(0, tn, "t1f", "t1u", 0)
+        xg(1, "t1u", 0)
+        compare(0, a0u, 2)
+        choose(0, tn, "t1f", "t1u", 1)
+        xg(1, "t1u", 1)
+        compare(1, a1u, 0)
+        choose(0, tn, "t1f", "t1u", 2)
+        xg(1, "t1u", 2)
+        compare(1, a1u, 1)
+        choose(1, "t1f", t2f, t2u, 0)
+        x2g(0)
+        compare(1, a1u, 2)
+        choose(1, "t1f", t2f, t2u, 1)
+        x2g(1)
+        filler[2]()
+        choose(1, "t1f", t2f, t2u, 2)
+        x2g(2)
+
+    def scan(j):
+        x, r, o = [col(b, 16 * CUTS[j], 16 * CUTS[j + 1]) for b in ("x2", "rm", "sc")]
+        V([x[1], r[1]], [o[1]], lambda: v.tensor_tensor_scan(o[0], r[0], x[0], 0.0, A.mult, A.max))
+
+    def shifted(t, t2f):
+        S([full(t2f)], [full("tc")], lambda: s.activation(T.tc[:], T[t2f][:], AF.Identity, bias=77.0 * (t + 1)))
+
+    def weigh(wt):
+        run("p", [full("sc"), full(wt)], [("cn1", 0, NL)], lambda: te.matmul(T.cn1[:, 0:NL], T[wt][:], T.sc[:, 15:E:16], True, True))
+
+    def next_lots(t2f, tnu):
+        o, w = col(tnu), col("vs")
+        V([("cn1", 0, NL)], [full("ui")], vc(T.ui[:], T.cn1[:, 0:NL]))
+        V([full("ui")], [full("uj")], v1(T.uj[:], T.ui[:], 1023, A.bitwise_and))
+        V([full("uj")], [w[1]], v2(w[0], T.uj[:], 2.0, 1.0, A.mult, A.add))
+        V([w[1], full(t2f)], [full("pr")], vt(T.pr[:], w[0], T[t2f][:], A.mult))
+        V([full("pr")], [full("ps")], v1(T.ps[:], T.pr[:], 5, A.logical_shift_right))
+        V([full("ps"), full("tc")], [full("sm")], vt(T.sm[:], T.ps[:], T.tc[:], A.add))
+        V([full("sm")], [full("tn")], v1(T.tn[:], T.sm[:], 4095, A.bitwise_and))
+        V([full("tn")], [o[1]], vc(o[0], T.tn[:]))
+
+    def bound():
+        run("p", [full("mk0"), full("mk1"), full("bo"), full("nb")], [("cn1", 0, NL)],
+            lambda: te.matmul(T.cn1[:, 0:NL], T.bo[:], T.mk0[:], True, False),
+            lambda: te.matmul(T.cn1[:, 0:NL], T.nb[:], T.mk1[:], False, True))
+        V([("cn1", 0, NL)], [full("sel")], v1(T.sel[:], T.cn1[:, 0:NL], 0.5, A.is_ge))
+
+    def pick(first, second, out):
+        f, z, o, d, p = col(first), col(second), col(out), col("vs"), col(("vs", NL))
+        V([f[1], z[1]], [d[1]], vt(d[0], f[0], z[0], A.subtract))
+        V([d[1], full("sel")], [p[1]], vt(p[0], d[0], T.sel[:], A.mult))
+        V([p[1], z[1]], [o[1]], vt(o[0], p[0], z[0], A.add))
+
+    def claim_rows(t, t2f):
+        run("p", [full(t2f), full("ts"), full("onef")], [("cn0", 0, NL)],
+            lambda: te.matmul(T.cn0[:, 0:NL], T.onef[0:1, 0:128], T.onef[0:1, 0:NL], True, False),
+            lambda: te.matmul(T.cn0[:, 0:NL], T.ts[:, 128 * t:128 * t + 128], T[t2f][:], False, True))
+
+    def claim_list(t):
+        rm = ("rm", 0, NL)
+        V([("cn0", 0, NL), full("dm")], [full("cmk")], vt(T.cmk[:], T.cn0[:, 0:NL], T.dm[:], A.mult))
+        V([full("cmk"), rm], [full("cs1")], lambda: v.tensor_tensor_scan(T.cs1[:], T.rm[:, 0:NL], T.cmk[:], 0.0, A.mult, A.add))
+        V([("cn0", 0, NL), full("cs1")], [full("cse")], vt(T.cse[:], T.cn0[:, 0:NL], T.cs1[:], A.is_equal))
+        V([full("cse"), rm], [full("cs2")], lambda: v.tensor_tensor_scan(T.cs2[:], T.rm[:, 0:NL], T.cse[:], 0.0, A.mult, A.add))
+        V([full("cs2")], [full("ct1")], v2(T.ct1[:], T.cs2[:, 15:NL:16], 8192.0, -8193.0, A.mult, A.add))
+        V([full("ct1"), full("cs1")], [full("ct2")], vt(T.ct2[:], T.ct1[:], T.cs1[:, 15:NL:16], A.add))
+        if t == 0:
+            V([full("ct2"), full("pcf")], [full("vl")], v1(T.vl[:], T.ct2[:], T.pcf[:, 3:4], A.min))
+        V([full("ct2"), full("pcf")], [full("of")], v1(T.of[:, 0:24:2], T.ct2[:], T.pcf[:, 3:4], A.min))
+
+    def scatter(t):
+        w = "w%d" % t
+        for c in range(12):
+            if t == 0:
+                src, rg = col("v0", 16 * c, 16 * c + 16)
+            else:
+                src, rg = T.x2[:, 256 * c + t:256 * c + 256:16], ("x2", 256 * c, 256 * c + 256)
+            V([rg, full("of")], [(w, 0, WW)], vc(T[w][:, 0:WW].indirect(T.of[:, 2 * c:2 * c + 1]), src))
+
+    def floor_const(i):
+        db = "db%d" % (i % 5)
+        run("p", [full("cstb"), full("oneb")], [(db, 0, 512)], lambda: te.matmul(T[db][:], T.cstb[0:1, :], T.oneb[0:1, :], True, False))
+
+    def sums(t, i):
+        db, w = "db%d" % (i % 5), "w%d" % t
+        run("p", [(w, 0, WW), full("qm")], [(db, 0, 512)],
+            lambda: te.matmul(T[db][:], T.qm[:], T[w][:, 512 * i:512 * i + 512], False, True))
+
+    def rise(t, i):
+        db, lo, hi = "db%d" % (i % 5), 512 * i, 512 * i + 512
+        V([(db, 0, 512), ("u", lo, hi)], [("u", lo, hi)], vt(T.u[:, lo:hi], T[db][:], T.u[:, lo:hi], A.add))
+        S([("u", lo, hi)], [("c", lo, hi)], lambda: s.activation(T.c[:, lo:hi], T.u[:, lo:hi], AF.Relu, bias=MAGIC + 255.0, scale=-1.0))
+        if i < 3:
+            floor_const(i + 5)
+            sums(t, i + 5)
+
+    def nothing():
+        pass
+
+    send("cst")
+    send_wide("pri")
+    step1("ph", True, "tu0", "lt", "a0u", ("pk", 1344), "a1u", "a1f", ("nsl", 0), "t2f0", "t2u0",
+          [more_constants, second_package, lambda: scan(0)])
+    stage("t2", T.t2u0[:], [full("t2u0")])
+    send("t2")
+    own("t2")
+    shifted(0, "t2f0")
+    bound()
+    pick(("pk", 1344), "a1f", "b1f")
+    V([full("b1f")], [("m4u", NL, 2 * NL)], vc(T.m4u[:, NL:2 * NL], T.b1f[:]))
+    pick("pb0", "pnr", "par0")
+    V([full("par0")], [("m4u", 2 * NL, 3 * NL)], vc(T.m4u[:, 2 * NL:3 * NL], T.par0[:]))
+    scan(1)
+    scan(2)
+    weigh("wth")
+    next_lots("t2f0", ("m4u", 0))
+    stage("m4", T.m4u[:], [full("m4u")])
+    send("m4")
+    own("m4")
+    for w in ("w1", "w2"):
+        iota(w, 0, WW, [[0, WW]], 0, 0, **small)
+    take("y", "cst", T.cso[:], [full("cso")])
+    take("y", "t2", T.o2u[:], [full("o2u")])
+    take("s", "pri", T.pl[:], [full("pl")])
+    V([("pcf", 1, 2), full("cm")], [full("dm")], v1(T.dm[:], T.cm[:], T.pcf[:, 1:2], A.is_equal))
+    V([("pcf", 1, 2), full("cm")], [full("eq")], v1(T.eq[:], T.cm[:, 0:128], T.pcf[:, 1:2], A.is_equal))
+    V([full("eq"), full("bo")], [full("idm")], vt(T.idm[:], T.eq[:], T.bo[:], A.mult))
+    V([full("eq"), full("idm")], [full("qk")], vt(T.qk[:], T.eq[:], T.idm[:], A.subtract))
+    for t in range(3):
+        V([full("bo"), ("pcf", 4 + t, 5 + t)], [("ts", 128 * t, 128 * t + 128)],
+          v1(T.ts[:, 128 * t:128 * t + 128], T.bo[:], T.pcf[:, 4 + t:5 + t], A.mult))
+    fill("onef", 0, NL, 1.0)
+    fill("oneb", 0, 512, 1.0)
+    fill("cstb", 0, 128, -63.0 / 128.0)
+    fill("u", W, WW, MAGIC)
+    V([full("cso")], [full("cof")], vc(T.cof[:], T.cso[:]))
+    V([full("idm"), full("cof")], [full("dg")], v2(T.dg[:], T.idm[:], T.cof[:, 3:4], 1.0 / 64.0, A.mult, A.mult))
+    run("p", [full("qk"), full("dg")], [("cn0", 0, 128)], lambda: te.matmul(T.cn0[:, 0:128], T.qk[:], T.dg[:], True, True))
+    V([("cn0", 0, 128)], [full("qm")], vc(T.qm[:], T.cn0[:, 0:128]))
+    V([full("bo"), full("cof")], [full("wto")], v1(T.wto[:], T.bo[:], T.cof[:, 4:5], A.mult))
+    for i in range(5):
+        floor_const(i)
+    for h in range(2):
+        (o, ro), (p, rp) = col("u", 2048 * h, 2048 * h + 2048), col("pl", 2048 * h, 2048 * h + 2048)
+        S([rp], [ro], lambda o=o, p=p: s.activation(o, p, AF.Identity, bias=MAGIC))
+    V([full("o2u")], [full("o2f")], vc(T.o2f[:], T.o2u[:]))
+    claim_rows(0, "o2f")
+    claim_list(0)
+    S([("u", 0, WW), full("vl")], [full("v0")], lambda: s.activation(T.v0[:], T.u[:, 0:WW].indirect(T.vl[:, 0:12]), AF.Identity, bias=-MAGIC))
+    scatter(0)
+    take("y", "m4", T.mo[:], [full("mo")])
+    for i in range(5):
+        sums(0, i)
+    for i in range(8):
+        rise(0, i)
+    V([full("mo")], [full("mof")], vc(T.mof[:], T.mo[:]))
+    dma("y", T.yh[:, 0:NL], T.t2f0[:], [full("t2f0")], [])
+    dma("y", T.yv[:, 0:NL], T.par0[0:128:16, :], [full("par0")], [])
+    for i in range(5):
+        floor_const(i)
+    step1("c", False, "mo", "mof", "o2u", "o2f", ("mo", NL), ("mof", NL), ("cof", 1), "t2f1", "t2u1", [nothing, nothing, lambda: scan(0)])
+    claim_rows(1, "t2f1")
+    shifted(1, "t2f1")
+    stage("y1", T.t2f1[:], [full("t2f1")])
+    send("y1")
+    own("y1")
+    claim_list(1)
+    scatter(1)
+    scan(1)
+    scan(2)
+    for i in range(2):
+        sums(1, i)
+    weigh("wto")
+    for i in range(2, 5):
+        sums(1, i)
+    for i in range(8):
+        rise(1, i)
+        if i == 3:
+            next_lots("t2f1", "tnu")
+    bound()
+    pick("o2f", ("mof", NL), "b1f")
+    V([full("b1f")], [full("b1u")], vc(T.b1u[:], T.b1f[:]))
+    pick("pb1", ("mof", 2 * NL), "par12")
+    take("y", "y1", T.yh[:, NL:2 * NL], [])
+    for i in range(5):
+        floor_const(i)
+    step1("c", False, "tnu", "tn", "t2u1", "t2f1", "b1u", "b1f", ("cof", 2), "t2f2", "t2u2", [nothing, nothing, nothing])
+    claim_rows(2, "t2f2")
+    stage("y2", T.t2f2[:], [full("t2f2")])
+    send("y2")
+    own("y2")
+    claim_list(2)
+    scatter(2)
+    for i in range(5):
+        sums(2, i)
+
+    def ship(b):
+        (c, rc), (p, rp) = col("c", BLOCKS[b], BLOCKS[b + 1]), col("pf", BLOCKS[b], BLOCKS[b + 1])
+        V([rc], [rp], v2(p, c, -1.0, 255.0, A.mult, A.add))
+        stage("o%d" % b, p, [rp])
+        send("o%d" % b)
+        own("o%d" % b)
+    nxt = 0
+    for i in range(8):
+        rise(2, i)
+        if nxt < NB - 1 and BLOCKS[nxt + 1] <= 512 * i:
+            ship(nxt)
+            nxt += 1
+    while nxt < NB:
+        ship(nxt)
+        nxt += 1
+    bound()
+    pick("pb2", "par12", ("par12", NL))
+    stage("par", T.par12[0:128:16, :], [full("par12")])
+    send("par")
+    own("par")
+    take("s", "y2", T.yh[:, 2 * NL:3 * NL], [])
+    for b in range(NB):
+        take("y", "o%d" % b, T.yp[:, BLOCKS[b]:BLOCKS[b + 1]], [])
+    take("s", "par", T.yv[:, NL:3 * NL], [])
+    for sem in sorted(total):
+        if seen.get(sem, 0) < total[sem]:
+            wait("g", sem, total[sem])

@@ -16,12 +16,12 @@ SCRATCH = {}
 for _d, _n, _names in (
         ("bfloat16", W, "ph c pl pf"), ("bfloat16", WW, "w0 w1 w2"), ("float32", WW, "u"), ("int32", 1536, "pk"),
         ("int32", NL, "lt pnr ui uj pr ps sm tn"), ("int32", 12, "pvi"), ("uint16", 24, "pvo of"), ("uint16", 12, "vl"),
-        ("int32", 8, "cs cso pci"), ("float32", 8, "csf nsl cof pcf"), ("float32", 128, "cd"), ("float32", 384, "ts par12"),
+        ("int32", 8, "cs cso pci"), ("float32", 8, "csf nsl cof pcf"), ("float32", 128, "cd"), ("float32", 384, "ts par12 at tt q0 q1 q2"),
         ("bfloat16", 128, "bo nb eq idm qk dg qm wth wto cstb"), ("bfloat16", 512, "oneb"), ("bfloat16", 2048, "sel16"),
-        ("bfloat16", E, "rm ind x2 sc"), ("float32", E, "xs0 xs1"), ("bfloat16", NL, "mk0 mk1 cse v0"),
-        ("float32", NL, "cm dm onef pb0 pb1 pb2 a1f sel t1f t2f0 t2f1 t2f2 o2f par0 b1f tc cmk cs1 cs2"),
+        ("bfloat16", E, "rm ind x2 sc"), ("float32", E, "xs0 xs1"), ("bfloat16", NL, "cse v0"), ("bfloat16", 384, "mk0 mk1"),
+        ("float32", NL, "cm dm onef pb0 pb1 pb2 a1f sel tf o2f par0 b1f tc cmk cs1 cs2"),
         ("uint16", NL, "tu0 a0u a1u t1u t2u0 t2u1 t2u2 o2u b1u tnu"), ("float32", 12, "ct1 ct2"),
-        ("uint16", 576, "m4u mo"), ("float32", 576, "mof")):
+        ("uint16", 576, "m4u mo"), ("float32", 384, "mof")):
     for _k in _names.split():
         SCRATCH[_k] = ("sbuf", [128, _n], _d)
 MSG = []
@@ -104,8 +104,11 @@ def rank_program(g, core, T, topo):
         return (name, 0, 1 << 20)
 
     def col(x, lo=0, hi=NL):
-        b, o = (x, 0) if x in SCRATCH else x
-        return T[b][:, o + lo:o + hi], (b, o + lo, o + hi)
+        if x in SCRATCH:
+            x = (x, 0)
+        b, st = x[0], x[2] if len(x) > 2 else 1
+        i, j = x[1] + lo * st, x[1] + (hi - 1) * st + 1
+        return (T[b][:, i:j] if st == 1 else T[b][:, i:j:st]), (b, i, j)
 
     def V(reads, writes, f):
         run("v", reads, writes, f)
@@ -127,8 +130,17 @@ def rank_program(g, core, T, topo):
     def v2(out, in0, s1, s2, op0, op1):
         return lambda: v.tensor_scalar(out, in0, s1, s2, op0, op1)
 
+    def copy(out, in_):
+        V([in_[1]], [out[1]], vc(out[0], in_[0]))
+
     def fill(b, lo, hi, x):
         V([], [(b, lo, hi)], lambda: v.memset(T[b][:, lo:hi], x))
+
+    def weave(*chains):
+        for i in range(max(len(c) for c in chains)):
+            for c in chains:
+                if i < len(c):
+                    c[i]()
 
     others = [(rank + j) % N for j in range(1, N)]
     away = [d for d in others if topo.chip(cores[d]) != topo.chip(core)]
@@ -163,11 +175,11 @@ def rank_program(g, core, T, topo):
         total["ar_" + m] = arrive[m]
         wait(q, "ar_" + m, arrive[m])
 
-    def stage(m, in_, reads):
-        dma("y", T["s_" + m][:], in_, reads, [full("s_" + m)])
+    mine = slice(16 * rank, 16 * rank + 16)
 
-    def own(m):
-        dma("y", T["l_" + m][rank], T["s_" + m][rank], [full("s_" + m)], [full("l_" + m)])
+    def stage(m, in_, reads, rows=None):
+        dma("y", T["s_" + m][:], in_[:] if rows is None else in_[0:128:16, :], reads, [full("s_" + m)])
+        dma("y", T["l_" + m][rank], in_[mine, :] if rows is None else in_[16 * rank:16 * rank + 1, :], reads, [full("l_" + m)])
 
     def take(q, m, out, writes):
         landed(q, m)
@@ -175,19 +187,19 @@ def rank_program(g, core, T, topo):
 
     fill("cs", 0, 8, 0)
     fill("pnr", 0, NL, 0)
-    dma("y", T.ph[:], T.price[:], [], [full("ph")])
+    fill("mk0", 0, 384, 0.0)
+    fill("mk1", 0, 384, 0.0)
     dma("s", T.lt[:], T.lots[:], [], [full("lt")])
-    dma("s", T.cs[:, 0:3], T.slack[:], [], [("cs", 0, 3)])
+    dma("y", T.cs[:, 0:3], T.slack[:], [], [("cs", 0, 3)])
+    dma("y", T.cs[:, 3:4], T.inc[:], [], [("cs", 3, 4)])
+    dma("y", T.cs[:, 4:5], T.wt[:], [], [("cs", 4, 5)])
     dma("s", T.pk[:, 1344:1536], T.packs[:, 1344:1536], [], [("pk", 1344, 1536)])
     dma("s", T.pvi[:], T.prev[:, 1344:1536], [], [full("pvi")])
+    dma("y", T.ph[:], T.price[:], [], [full("ph")])
+    dma("s", T.pnr[0:128:16, :], T.prev[:, 1344:1536], [], [full("pnr")])
     dma("y", T.pk[:, 0:1344], T.packs[:, 0:1344], [], [("pk", 0, 1344)])
-    dma("s", T.cs[:, 3:4], T.inc[:], [], [("cs", 3, 4)])
-    dma("s", T.cs[:, 4:5], T.wt[:], [], [("cs", 4, 5)])
-    stage("pri", T.price[:], [])
-    dma("y", T.pnr[0:128:16, :], T.prev[:, 1344:1536], [], [full("pnr")])
-    stage("cst", T.cs[:], [full("cs")])
-    own("pri")
-    own("cst")
+    stage("pri", T.price, [])
+    stage("cst", T.cs, [full("cs")])
 
     def iota(b, lo, hi, pat, base, cm, **kw):
         run("g", [], [(b, lo, hi)], lambda: g.iota(T[b][:, lo:hi], pat, base, cm, **kw))
@@ -199,24 +211,24 @@ def rank_program(g, core, T, topo):
         iota("pb%d" % t, 0, NL, [[1, NL]], 1344 + NL * t, 0, **small)
     V([("pci", 0, 1)], [("pci", 1, 2)], v1(T.pci[:, 1:2], T.pci[:, 0:1], 15, A.bitwise_and))
     V([("pci", 0, 1)], [("pci", 2, 3)], v1(T.pci[:, 2:3], T.pci[:, 0:1], 4, A.logical_shift_right))
+    fill("sel16", 0, 2048, 0.0)
     V([("pci", 1, 3)], [("pcf", 1, 3)], vc(T.pcf[:, 1:3], T.pci[:, 1:3]))
+    copy(col("tu0"), col("lt"))
+    copy(col("tt", 0, 8), col("cs", 0, 8)) if False else copy(col("csf", 0, 8), col("cs", 0, 8))
+    V([full("cd"), ("pcf", 2, 3)], [full("bo")], v1(T.bo[:], T.cd[:], T.pcf[:, 2:3], A.is_equal))
+    V([full("csf")], [full("nsl")], v1(T.nsl[:], T.csf[:], -1.0, A.mult))
     V([("pcf", 1, 2)], [("pcf", 3, 4)], v1(T.pcf[:, 3:4], T.pcf[:, 1:2], float(W), A.add))
     for t in range(3):
         V([("pcf", 1, 2)], [("pcf", 4 + t, 5 + t)], v1(T.pcf[:, 4 + t:5 + t], T.pcf[:, 1:2], float(t), A.is_equal))
-    V([full("cd"), ("pcf", 2, 3)], [full("bo")], v1(T.bo[:], T.cd[:], T.pcf[:, 2:3], A.is_equal))
-    fill("sel16", 0, 2048, 0.0)
-    V([full("lt")], [full("tu0")], vc(T.tu0[:], T.lt[:]))
-    V([full("cs")], [full("csf")], vc(T.csf[:], T.cs[:]))
-    V([full("csf")], [full("nsl")], v1(T.nsl[:], T.csf[:], -1.0, A.mult))
     for k in range(16):
         V([full("bo")], [("sel16", 128 * k, 128 * k + 128)], vc(T.sel16[:, 128 * k + k:128 * k + 128:16], T.bo[:, 0:128:16]))
-    V([("pk", 1344, 1536)], [full("a0u")], vc(T.a0u[:], T.pk[:, 1344:1536]))
+    copy(col("a0u"), col(("pk", 1344)))
 
     def more_constants():
         V([full("bo")], [full("nb")], v1(T.nb[:], T.bo[:], -17.0, A.mult))
         fill("rm", 0, E, 1.0)
-        V([full("rm")], [full("rm")], lambda: v.memset(T.rm[:, 0:E:16], 0.0))
         V([full("bo"), full("csf")], [full("wth")], v1(T.wth[:], T.bo[:], T.csf[:, 4:5], A.mult))
+        V([full("rm")], [full("rm")], lambda: v.memset(T.rm[:, 0:E:16], 0.0))
         fill("w0", 0, WW, 0.0)
 
     def second_package():
@@ -225,7 +237,10 @@ def rank_program(g, core, T, topo):
             V([full("pvo"), full("pk")], [("a1f", c, c + 1)], vc(T.a1f[:, c:NL:12], T.pk[:, 0:1536].indirect(T.pvo[:, 2 * c:2 * c + 1])))
         V([full("a1f")], [full("a1u")], vc(T.a1u[:], T.a1f[:]))
 
-    def step1(tab, low, tu, tn, a0u, a0n, a1u, a1n, bias, t2f, t2u, filler):
+    ODD, EVEN = 1, 0
+    BANK_OF = [0, 1, 0, 1, 0, 1]
+
+    def step1(tab, low, tu, tn, a0u, a0n, a1u, a1n, bias, q, t2u, filler):
         def lanes(x, j):
             return col(x, CUTS[j], CUTS[j + 1])
 
@@ -240,23 +255,24 @@ def rank_program(g, core, T, topo):
         def compare(tr, lst, j):
             l, x, o, n = lanes(lst, j), items("xs%d" % tr, j), items("ind", j), CUTS[j + 1] - CUTS[j]
             V([full(tab), l[1], x[1]], [o[1]], vt(o[0], T[tab][:, 0:W].indirect(l[0]), x[0], A.is_lt if low else A.is_gt))
-            cn = "cn%d" % ((tr * 3 + j) % 2)
+            cn = "cn%d" % BANK_OF[tr * 3 + j]
             run("p", [o[1], full("sel16")], [(cn, 0, n)],
                 *[(lambda k=k: te.matmul(T[cn][:, 0:n], T.sel16[:, 128 * k:128 * k + 128], T.ind[:, o[1][1] + k:o[1][2]:16],
                                          k == 0, k == 15)) for k in range(16)])
 
-        def choose(tr, cur, newf, newu, j):
+        def choose(tr, j):
             n = CUTS[j + 1] - CUTS[j]
-            cn = "cn%d" % ((tr * 3 + j) % 2)
-            m, d, p = lanes("mk%d" % tr, j), lanes("vs", j), lanes(("vs", NL), j)
-            c, f, u = lanes(cur, j), lanes(newf, j), lanes(newu, j)
+            cn, mk = "cn%d" % BANK_OF[tr * 3 + j], "mk%d" % tr
+            src, out, lst = ("at", "tt", "t1u") if tr == 0 else ("tt", q, t2u)
+            m, u = lanes((mk, ODD, 2), j), lanes(lst, j)
+            (k, rk), (i, ri), (o, ro) = [col(b, 2 * CUTS[j], 2 * CUTS[j + 1]) for b in (mk, src, out)]
+            new = lanes((out, ODD, 2), j)
             V([(cn, 0, n)], [m[1]], v1(m[0], T[cn][:, 0:n], 8.5, A.is_ge))
-            V([d[1], m[1]], [p[1]], vt(p[0], d[0], m[0], A.mult))
-            V([p[1], c[1]], [f[1]], vt(f[0], p[0], c[0], A.add))
-            V([f[1]], [u[1]], vc(u[0], f[0]))
+            V([rk, ri], [ro], lambda: v.tensor_tensor_scan(o, k, i, 0.0, A.mult, A.add))
+            copy(u, new)
             if tr == 0:
-                a = lanes(a1n, j)
-                V([a[1], f[1]], [d[1]], vt(d[0], a[0], f[0], A.subtract))
+                a, d = lanes(a1n, j), lanes((out, EVEN, 2), j)
+                V([a[1], ro], [ro], vt(d[0], a[0], new[0], A.subtract))
 
         def x2g(j):
             l, o = lanes(t2u, j), items("x2", j)
@@ -265,88 +281,101 @@ def rank_program(g, core, T, topo):
 
         for j in range(3):
             xg(0, tu, j)
-        d, a, t = col("vs"), col(a0n), col(tn)
-        V([a[1], t[1]], [d[1]], vt(d[0], a[0], t[0], A.subtract))
+        t, a = col(tn), col(a0n)
+        V([t[1]], [("at", 1, 384)], vc(T.at[:, 1:384:2], t[0]))
+        V([a[1], t[1]], [("at", 0, 383)], vt(T.at[:, 0:383:2], a[0], t[0], A.subtract))
         filler[0]()
         compare(0, a0u, 0)
         filler[1]()
         compare(0, a0u, 1)
-        choose(0, tn, "t1f", "t1u", 0)
+        choose(0, 0)
         xg(1, "t1u", 0)
         compare(0, a0u, 2)
-        choose(0, tn, "t1f", "t1u", 1)
+        choose(0, 1)
         xg(1, "t1u", 1)
         compare(1, a1u, 0)
-        choose(0, tn, "t1f", "t1u", 2)
+        choose(0, 2)
         xg(1, "t1u", 2)
         compare(1, a1u, 1)
-        choose(1, "t1f", t2f, t2u, 0)
+        choose(1, 0)
         x2g(0)
         compare(1, a1u, 2)
-        choose(1, "t1f", t2f, t2u, 1)
+        choose(1, 1)
         x2g(1)
         filler[2]()
-        choose(1, "t1f", t2f, t2u, 2)
-        x2g(2)
+        choose(1, 2)
+
+    def last_x2(tab, low, t2u):
+        kw = {} if low else {"scale": -1.0, "bias": 255.0}
+        l, o = col(t2u, CUTS[2], NL), col("x2", 16 * CUTS[2], E)
+        S([full(tab), l[1]], [o[1]], lambda: s.activation(o[0], T[tab][:, 0:W].indirect(l[0]), AF.Identity, **kw))
 
     def scan(j):
         x, r, o = [col(b, 16 * CUTS[j], 16 * CUTS[j + 1]) for b in ("x2", "rm", "sc")]
         V([x[1], r[1]], [o[1]], lambda: v.tensor_tensor_scan(o[0], r[0], x[0], 0.0, A.mult, A.max))
 
-    def shifted(t, t2f):
-        S([full(t2f)], [full("tc")], lambda: s.activation(T.tc[:], T[t2f][:], AF.Identity, bias=77.0 * (t + 1)))
+    def lots_of(q):
+        S([(q, 0, 384)], [full("tf")], lambda: s.activation(T.tf[:], T[q][:, 1:384:2], AF.Identity))
+
+    def shifted(t, q):
+        S([(q, 0, 384)], [full("tc")], lambda: s.activation(T.tc[:], T[q][:, 1:384:2], AF.Identity, bias=77.0 * (t + 1)))
 
     def weigh(wt):
         run("p", [full("sc"), full(wt)], [("cn1", 0, NL)], lambda: te.matmul(T.cn1[:, 0:NL], T[wt][:], T.sc[:, 15:E:16], True, True))
 
-    def next_lots(t2f, tnu):
-        o, w = col(tnu), col("vs")
-        V([("cn1", 0, NL)], [full("ui")], vc(T.ui[:], T.cn1[:, 0:NL]))
-        V([full("ui")], [full("uj")], v1(T.uj[:], T.ui[:], 1023, A.bitwise_and))
-        V([full("uj")], [w[1]], v2(w[0], T.uj[:], 2.0, 1.0, A.mult, A.add))
-        V([w[1], full(t2f)], [full("pr")], vt(T.pr[:], w[0], T[t2f][:], A.mult))
-        V([full("pr")], [full("ps")], v1(T.ps[:], T.pr[:], 5, A.logical_shift_right))
-        V([full("ps"), full("tc")], [full("sm")], vt(T.sm[:], T.ps[:], T.tc[:], A.add))
-        V([full("sm")], [full("tn")], v1(T.tn[:], T.sm[:], 4095, A.bitwise_and))
-        V([full("tn")], [o[1]], vc(o[0], T.tn[:]))
+    def next_lots(q, tnu):
+        o, w, t2 = col(tnu), col("vs"), col((q, ODD, 2))
+        return [lambda: V([("cn1", 0, NL)], [full("ui")], vc(T.ui[:], T.cn1[:, 0:NL])),
+                lambda: V([full("ui")], [full("uj")], v1(T.uj[:], T.ui[:], 1023, A.bitwise_and)),
+                lambda: V([full("uj")], [w[1]], v2(w[0], T.uj[:], 2.0, 1.0, A.mult, A.add)),
+                lambda: V([w[1], t2[1]], [full("pr")], vt(T.pr[:], w[0], t2[0], A.mult)),
+                lambda: V([full("pr")], [full("ps")], v1(T.ps[:], T.pr[:], 5, A.logical_shift_right)),
+                lambda: V([full("ps"), full("tc")], [full("sm")], vt(T.sm[:], T.ps[:], T.tc[:], A.add)),
+                lambda: V([full("sm")], [full("tn")], v1(T.tn[:], T.sm[:], 4095, A.bitwise_and)),
+                lambda: V([full("tn")], [o[1]], vc(o[0], T.tn[:]))]
 
     def bound():
         run("p", [full("mk0"), full("mk1"), full("bo"), full("nb")], [("cn1", 0, NL)],
-            lambda: te.matmul(T.cn1[:, 0:NL], T.bo[:], T.mk0[:], True, False),
-            lambda: te.matmul(T.cn1[:, 0:NL], T.nb[:], T.mk1[:], False, True))
+            lambda: te.matmul(T.cn1[:, 0:NL], T.bo[:], T.mk0[:, 1:384:2], True, False),
+            lambda: te.matmul(T.cn1[:, 0:NL], T.nb[:], T.mk1[:, 1:384:2], False, True))
         V([("cn1", 0, NL)], [full("sel")], v1(T.sel[:], T.cn1[:, 0:NL], 0.5, A.is_ge))
 
-    def pick(first, second, out):
-        f, z, o, d, p = col(first), col(second), col(out), col("vs"), col(("vs", NL))
-        V([f[1], z[1]], [d[1]], vt(d[0], f[0], z[0], A.subtract))
-        V([d[1], full("sel")], [p[1]], vt(p[0], d[0], T.sel[:], A.mult))
-        V([p[1], z[1]], [o[1]], vt(o[0], p[0], z[0], A.add))
+    def pick(first, second, out, c0):
+        f, z, o, d = col(first), col(second), col(out), col(("vs", c0))
+        return [lambda: V([f[1], z[1]], [d[1]], vt(d[0], f[0], z[0], A.subtract)),
+                lambda: V([d[1], full("sel")], [d[1]], vt(d[0], d[0], T.sel[:], A.mult)),
+                lambda: V([d[1], z[1]], [o[1]], vt(o[0], d[0], z[0], A.add))]
 
-    def claim_rows(t, t2f):
-        run("p", [full(t2f), full("ts"), full("onef")], [("cn0", 0, NL)],
-            lambda: te.matmul(T.cn0[:, 0:NL], T.onef[0:1, 0:128], T.onef[0:1, 0:NL], True, False),
-            lambda: te.matmul(T.cn0[:, 0:NL], T.ts[:, 128 * t:128 * t + 128], T[t2f][:], False, True))
+    def claim_ones():
+        run("p", [full("onef")], [("cn0", 0, NL)], lambda: te.matmul(T.cn0[:, 0:NL], T.onef[0:1, 0:128], T.onef[0:1, 0:NL], True, False))
+
+    def claim_rows(t, t2):
+        x = col(t2)
+        run("p", [x[1], full("ts"), full("onef")], [("cn0", 0, NL)],
+            lambda: te.matmul(T.cn0[:, 0:NL], T.ts[:, 128 * t:128 * t + 128], x[0], False, True))
 
     def claim_list(t):
         rm = ("rm", 0, NL)
-        V([("cn0", 0, NL), full("dm")], [full("cmk")], vt(T.cmk[:], T.cn0[:, 0:NL], T.dm[:], A.mult))
-        V([full("cmk"), rm], [full("cs1")], lambda: v.tensor_tensor_scan(T.cs1[:], T.rm[:, 0:NL], T.cmk[:], 0.0, A.mult, A.add))
-        V([("cn0", 0, NL), full("cs1")], [full("cse")], vt(T.cse[:], T.cn0[:, 0:NL], T.cs1[:], A.is_equal))
-        V([full("cse"), rm], [full("cs2")], lambda: v.tensor_tensor_scan(T.cs2[:], T.rm[:, 0:NL], T.cse[:], 0.0, A.mult, A.add))
-        V([full("cs2")], [full("ct1")], v2(T.ct1[:], T.cs2[:, 15:NL:16], 8192.0, -8193.0, A.mult, A.add))
-        V([full("ct1"), full("cs1")], [full("ct2")], vt(T.ct2[:], T.ct1[:], T.cs1[:, 15:NL:16], A.add))
-        if t == 0:
-            V([full("ct2"), full("pcf")], [full("vl")], v1(T.vl[:], T.ct2[:], T.pcf[:, 3:4], A.min))
-        V([full("ct2"), full("pcf")], [full("of")], v1(T.of[:, 0:24:2], T.ct2[:], T.pcf[:, 3:4], A.min))
+        return [
+            lambda: V([("cn0", 0, NL), full("dm")], [full("cmk")], vt(T.cmk[:], T.cn0[:, 0:NL], T.dm[:], A.mult)),
+            lambda: V([full("cmk"), rm], [full("cs1")], lambda: v.tensor_tensor_scan(T.cs1[:], T.rm[:, 0:NL], T.cmk[:], 0.0, A.mult, A.add)),
+            lambda: V([("cn0", 0, NL), full("cs1")], [full("cse")], vt(T.cse[:], T.cn0[:, 0:NL], T.cs1[:], A.is_equal)),
+            lambda: V([full("cse"), rm], [full("cs2")], lambda: v.tensor_tensor_scan(T.cs2[:], T.rm[:, 0:NL], T.cse[:], 0.0, A.mult, A.add)),
+            lambda: V([full("cs2")], [full("ct1")], v2(T.ct1[:], T.cs2[:, 15:NL:16], 8192.0, -8193.0, A.mult, A.add)),
+            lambda: V([full("ct1"), full("cs1")], [full("ct2")], vt(T.ct2[:], T.ct1[:], T.cs1[:, 15:NL:16], A.add))] + (
+            [lambda: V([full("ct2"), full("pcf")], [full("vl")], v1(T.vl[:], T.ct2[:], T.pcf[:, 3:4], A.min))] if t == 0 else []) + [
+            lambda: V([full("ct2"), full("pcf")], [full("of")], v1(T.of[:, 0:24:2], T.ct2[:], T.pcf[:, 3:4], A.min))]
 
     def scatter(t):
         w = "w%d" % t
-        for c in range(12):
+
+        def call(c):
             if t == 0:
                 src, rg = col("v0", 16 * c, 16 * c + 16)
             else:
                 src, rg = T.x2[:, 256 * c + t:256 * c + 256:16], ("x2", 256 * c, 256 * c + 256)
             V([rg, full("of")], [(w, 0, WW)], vc(T[w][:, 0:WW].indirect(T.of[:, 2 * c:2 * c + 1]), src))
+        return [lambda c=c: call(c) for c in range(12)]
 
     def floor_const(i):
         db = "db%d" % (i % 5)
@@ -368,109 +397,126 @@ def rank_program(g, core, T, topo):
     def nothing():
         pass
 
-    send("cst")
     send_wide("pri")
-    step1("ph", True, "tu0", "lt", "a0u", ("pk", 1344), "a1u", "a1f", ("nsl", 0), "t2f0", "t2u0",
+    send("cst")
+    step1("ph", True, "tu0", "lt", "a0u", ("pk", 1344), "a1u", "a1f", ("nsl", 0), "q0", "t2u0",
           [more_constants, second_package, lambda: scan(0)])
-    stage("t2", T.t2u0[:], [full("t2u0")])
+    stage("t2", T.t2u0, [full("t2u0")])
     send("t2")
-    own("t2")
-    shifted(0, "t2f0")
+    last_x2("ph", True, "t2u0")
+    shifted(0, "q0")
+    lots_of("q0")
+    take("y", "cst", T.cso[:], [full("cso")])
+    take("y", "t2", T.o2u[:], [full("o2u")])
+    dma("y", T.yh[:, 0:NL], T.tf[:], [full("tf")], [])
     bound()
-    pick(("pk", 1344), "a1f", "b1f")
-    V([full("b1f")], [("m4u", NL, 2 * NL)], vc(T.m4u[:, NL:2 * NL], T.b1f[:]))
-    pick("pb0", "pnr", "par0")
-    V([full("par0")], [("m4u", 2 * NL, 3 * NL)], vc(T.m4u[:, 2 * NL:3 * NL], T.par0[:]))
+    weave(pick(("pk", 1344), "a1f", "b1f", 0), pick("pb0", "pnr", "par0", NL))
+    copy(col(("m4u", NL)), col("b1f"))
+    copy(col(("m4u", 2 * NL)), col("par0"))
     scan(1)
     scan(2)
     weigh("wth")
-    next_lots("t2f0", ("m4u", 0))
-    stage("m4", T.m4u[:], [full("m4u")])
-    send("m4")
-    own("m4")
-    for w in ("w1", "w2"):
-        iota(w, 0, WW, [[0, WW]], 0, 0, **small)
-    take("y", "cst", T.cso[:], [full("cso")])
-    take("y", "t2", T.o2u[:], [full("o2u")])
-    take("s", "pri", T.pl[:], [full("pl")])
-    V([("pcf", 1, 2), full("cm")], [full("dm")], v1(T.dm[:], T.cm[:], T.pcf[:, 1:2], A.is_equal))
-    V([("pcf", 1, 2), full("cm")], [full("eq")], v1(T.eq[:], T.cm[:, 0:128], T.pcf[:, 1:2], A.is_equal))
-    V([full("eq"), full("bo")], [full("idm")], vt(T.idm[:], T.eq[:], T.bo[:], A.mult))
-    V([full("eq"), full("idm")], [full("qk")], vt(T.qk[:], T.eq[:], T.idm[:], A.subtract))
-    for t in range(3):
+
+    def c_dm():
+        V([("pcf", 1, 2), full("cm")], [full("dm")], v1(T.dm[:], T.cm[:], T.pcf[:, 1:2], A.is_equal))
+
+    def c_eq():
+        V([("pcf", 1, 2), full("cm")], [full("eq")], v1(T.eq[:], T.cm[:, 0:128], T.pcf[:, 1:2], A.is_equal))
+
+    def c_id():
+        V([full("eq"), full("bo")], [full("idm")], vt(T.idm[:], T.eq[:], T.bo[:], A.mult))
+
+    def c_qk():
+        V([full("eq"), full("idm")], [full("qk")], vt(T.qk[:], T.eq[:], T.idm[:], A.subtract))
+
+    def c_ts(t):
         V([full("bo"), ("pcf", 4 + t, 5 + t)], [("ts", 128 * t, 128 * t + 128)],
           v1(T.ts[:, 128 * t:128 * t + 128], T.bo[:], T.pcf[:, 4 + t:5 + t], A.mult))
-    fill("onef", 0, NL, 1.0)
-    fill("oneb", 0, 512, 1.0)
-    fill("cstb", 0, 128, -63.0 / 128.0)
+    weave([lambda: c_eq(), lambda: fill("onef", 0, NL, 1.0), lambda: c_id(), lambda: c_ts(0), lambda: c_qk(), lambda: c_dm(),
+           lambda: fill("cstb", 0, 128, -63.0 / 128.0), lambda: fill("oneb", 0, 512, 1.0)], next_lots("q0", ("m4u", 0)))
+    stage("m4", T.m4u, [full("m4u")])
+    send("m4")
+    for w in ("w1", "w2"):
+        iota(w, 0, WW, [[0, WW]], 0, 0, **small)
+    take("s", "pri", T.pl[:], [full("pl")])
+    claim_ones()
+    copy(col("cof", 0, 8), col("cso", 0, 8))
     fill("u", W, WW, MAGIC)
-    V([full("cso")], [full("cof")], vc(T.cof[:], T.cso[:]))
     V([full("idm"), full("cof")], [full("dg")], v2(T.dg[:], T.idm[:], T.cof[:, 3:4], 1.0 / 64.0, A.mult, A.mult))
-    run("p", [full("qk"), full("dg")], [("cn0", 0, 128)], lambda: te.matmul(T.cn0[:, 0:128], T.qk[:], T.dg[:], True, True))
-    V([("cn0", 0, 128)], [full("qm")], vc(T.qm[:], T.cn0[:, 0:128]))
+    run("p", [full("qk"), full("dg")], [("cn1", 0, 128)], lambda: te.matmul(T.cn1[:, 0:128], T.qk[:], T.dg[:], True, True))
+    c_ts(1)
+    c_ts(2)
     V([full("bo"), full("cof")], [full("wto")], v1(T.wto[:], T.bo[:], T.cof[:, 4:5], A.mult))
+    V([("cn1", 0, 128)], [full("qm")], vc(T.qm[:], T.cn1[:, 0:128]))
     for i in range(5):
         floor_const(i)
     for h in range(2):
         (o, ro), (p, rp) = col("u", 2048 * h, 2048 * h + 2048), col("pl", 2048 * h, 2048 * h + 2048)
         S([rp], [ro], lambda o=o, p=p: s.activation(o, p, AF.Identity, bias=MAGIC))
-    V([full("o2u")], [full("o2f")], vc(T.o2f[:], T.o2u[:]))
+    copy(col("o2f"), col("o2u"))
     claim_rows(0, "o2f")
-    claim_list(0)
+    weave(claim_list(0))
     S([("u", 0, WW), full("vl")], [full("v0")], lambda: s.activation(T.v0[:], T.u[:, 0:WW].indirect(T.vl[:, 0:12]), AF.Identity, bias=-MAGIC))
-    scatter(0)
+    weave(scatter(0))
     take("y", "m4", T.mo[:], [full("mo")])
     for i in range(5):
         sums(0, i)
     for i in range(8):
         rise(0, i)
-    V([full("mo")], [full("mof")], vc(T.mof[:], T.mo[:]))
-    dma("y", T.yh[:, 0:NL], T.t2f0[:], [full("t2f0")], [])
+    copy(col("mof", 0, 384), col(("mo", NL), 0, 384))
     dma("y", T.yv[:, 0:NL], T.par0[0:128:16, :], [full("par0")], [])
     for i in range(5):
         floor_const(i)
-    step1("c", False, "mo", "mof", "o2u", "o2f", ("mo", NL), ("mof", NL), ("cof", 1), "t2f1", "t2u1", [nothing, nothing, lambda: scan(0)])
-    claim_rows(1, "t2f1")
-    shifted(1, "t2f1")
-    stage("y1", T.t2f1[:], [full("t2f1")])
+
+    def scan_first():
+        scan(0)
+        claim_ones()
+    step1("c", False, "mo", "mo", "o2u", "o2f", ("mo", NL), "mof", ("cof", 1), "q1", "t2u1", [nothing, nothing, scan_first])
+    claim_rows(1, ("q1", ODD, 2))
+    last_x2("c", False, "t2u1")
+    shifted(1, "q1")
+    lots_of("q1")
+    stage("y1", T.tf, [full("tf")])
     send("y1")
-    own("y1")
-    claim_list(1)
-    scatter(1)
     scan(1)
+    cl = claim_list(1)
+    weave(cl[:4])
     scan(2)
-    for i in range(2):
-        sums(1, i)
     weigh("wto")
-    for i in range(2, 5):
+    weave(cl[4:])
+    weave(scatter(1), [nothing, nothing] + next_lots("q1", "tnu"))
+    for i in range(5):
         sums(1, i)
     for i in range(8):
         rise(1, i)
-        if i == 3:
-            next_lots("t2f1", "tnu")
     bound()
-    pick("o2f", ("mof", NL), "b1f")
-    V([full("b1f")], [full("b1u")], vc(T.b1u[:], T.b1f[:]))
-    pick("pb1", ("mof", 2 * NL), "par12")
+    weave(pick("o2f", "mof", "b1f", 0), pick("pb1", ("mof", NL), "par12", NL))
+    copy(col("b1u"), col("b1f"))
     take("y", "y1", T.yh[:, NL:2 * NL], [])
     for i in range(5):
         floor_const(i)
-    step1("c", False, "tnu", "tn", "t2u1", "t2f1", "b1u", "b1f", ("cof", 2), "t2f2", "t2u2", [nothing, nothing, nothing])
-    claim_rows(2, "t2f2")
-    stage("y2", T.t2f2[:], [full("t2f2")])
+    step1("c", False, "tnu", "tn", "t2u1", ("q1", ODD, 2), "b1u", "b1f", ("cof", 2), "q2", "t2u2", [nothing, nothing, claim_ones])
+    claim_rows(2, ("q2", ODD, 2))
+    last_x2("c", False, "t2u2")
+    lots_of("q2")
+    stage("y2", T.tf, [full("tf")])
     send("y2")
-    own("y2")
-    claim_list(2)
-    scatter(2)
+    bound()
+    weave(pick("pb2", "par12", ("par12", NL), 0))
+    stage("par", T.par12, [full("par12")], rows=True)
+    send("par")
+    weave(claim_list(2))
+    weave(scatter(2))
     for i in range(5):
         sums(2, i)
 
     def ship(b):
         (c, rc), (p, rp) = col("c", BLOCKS[b], BLOCKS[b + 1]), col("pf", BLOCKS[b], BLOCKS[b + 1])
         V([rc], [rp], v2(p, c, -1.0, 255.0, A.mult, A.add))
-        stage("o%d" % b, p, [rp])
-        send("o%d" % b)
-        own("o%d" % b)
+        m = "o%d" % b
+        dma("y", T["s_" + m][:], p, [rp], [full("s_" + m)])
+        dma("y", T["l_" + m][rank], T.pf[mine, BLOCKS[b]:BLOCKS[b + 1]], [rp], [full("l_" + m)])
+        send(m)
     nxt = 0
     for i in range(8):
         rise(2, i)
@@ -480,15 +526,10 @@ def rank_program(g, core, T, topo):
     while nxt < NB:
         ship(nxt)
         nxt += 1
-    bound()
-    pick("pb2", "par12", ("par12", NL))
-    stage("par", T.par12[0:128:16, :], [full("par12")])
-    send("par")
-    own("par")
     take("s", "y2", T.yh[:, 2 * NL:3 * NL], [])
-    for b in range(NB):
-        take("y", "o%d" % b, T.yp[:, BLOCKS[b]:BLOCKS[b + 1]], [])
     take("s", "par", T.yv[:, NL:3 * NL], [])
+    for b in range(NB):
+        take("s", "o%d" % b, T.yp[:, BLOCKS[b]:BLOCKS[b + 1]], [])
     for sem in sorted(total):
         if seen.get(sem, 0) < total[sem]:
             wait("g", sem, total[sem])

@@ -10,16 +10,16 @@ E = 16 * NL
 W = 4096
 WW = W + 16
 CUTS = [0, 64, 128, 192]
-BLOCKS = [0, 1024, 2048, 3072, W]
+BLOCKS = [0, 1024, 2048, 3072, 3584, W]
 NB = len(BLOCKS) - 1
 SCRATCH = {}
 for _d, _n, _names in (
-        ("bfloat16", W, "ph c pl pf"), ("bfloat16", WW, "w0 w1 w2"), ("float32", WW, "u"), ("int32", 1536, "pk"),
+        ("bfloat16", W, "ph c pf"), ("bfloat16", WW, "w0 w1 w2 pl"), ("float32", W, "dd"), ("int32", 1536, "pk"),
         ("int32", NL, "lt pnr ui uj pr ps sm tn"), ("int32", 12, "pvi"), ("uint16", 24, "pvo of"), ("uint16", 12, "vl"),
         ("int32", 8, "cs cso pci"), ("float32", 8, "csf nsl cof pcf"), ("float32", 128, "cd"), ("float32", 384, "ts par12 at tt q0 q1 q2"),
-        ("bfloat16", 128, "bo nb eq idm qk dg qm wth wto cstb"), ("bfloat16", 512, "oneb"), ("bfloat16", 2048, "sel16"),
+        ("bfloat16", 128, "bo nb eq idm nid qk dg qm wth wto cstb cst2"), ("bfloat16", 512, "oneb"), ("bfloat16", 2048, "sel16"),
         ("bfloat16", E, "rm ind x2 sc"), ("float32", E, "xs0 xs1"), ("bfloat16", NL, "cse v0"), ("bfloat16", 384, "mk0 mk1"),
-        ("float32", NL, "cm dm onef pb0 pb1 pb2 a1f sel tf o2f par0 b1f tc cmk cs1 cs2"),
+        ("float32", NL, "cm dm pb0 pb1 pb2 a1f sel tf o2f par0 b1f tc cmk cs1 cs2"),
         ("uint16", NL, "tu0 a0u a1u t1u t2u0 t2u1 t2u2 o2u b1u tnu"), ("float32", 12, "ct1 ct2"),
         ("uint16", 576, "m4u mo"), ("float32", 384, "mof")):
     for _k in _names.split():
@@ -66,7 +66,7 @@ def rank_program(g, core, T, topo):
             for e in hist.get(b, []):
                 over = e[0] < hi and lo < e[1]
                 if e[2] == q and not is_dma:
-                    need = over and e[5]
+                    need = over and (e[5] or (wr and bank))
                 else:
                     need = bank or (over and (wr or e[5]))
                 if need:
@@ -142,6 +142,9 @@ def rank_program(g, core, T, topo):
                 if i < len(c):
                     c[i]()
 
+    def nothing():
+        pass
+
     others = [(rank + j) % N for j in range(1, N)]
     away = [d for d in others if topo.chip(cores[d]) != topo.chip(core)]
     near = [d for d in others if topo.chip(cores[d]) == topo.chip(core)]
@@ -191,13 +194,13 @@ def rank_program(g, core, T, topo):
     fill("mk1", 0, 384, 0.0)
     dma("s", T.lt[:], T.lots[:], [], [full("lt")])
     dma("y", T.cs[:, 0:3], T.slack[:], [], [("cs", 0, 3)])
-    dma("y", T.cs[:, 3:4], T.inc[:], [], [("cs", 3, 4)])
-    dma("y", T.cs[:, 4:5], T.wt[:], [], [("cs", 4, 5)])
+    dma("y", T.ph[:], T.price[:], [], [full("ph")])
     dma("s", T.pk[:, 1344:1536], T.packs[:, 1344:1536], [], [("pk", 1344, 1536)])
     dma("s", T.pvi[:], T.prev[:, 1344:1536], [], [full("pvi")])
-    dma("y", T.ph[:], T.price[:], [], [full("ph")])
-    dma("s", T.pnr[0:128:16, :], T.prev[:, 1344:1536], [], [full("pnr")])
     dma("y", T.pk[:, 0:1344], T.packs[:, 0:1344], [], [("pk", 0, 1344)])
+    dma("s", T.cs[:, 3:4], T.inc[:], [], [("cs", 3, 4)])
+    dma("s", T.cs[:, 4:5], T.wt[:], [], [("cs", 4, 5)])
+    dma("s", T.pnr[0:128:16, :], T.prev[:, 1344:1536], [], [full("pnr")])
     stage("pri", T.price, [])
     stage("cst", T.cs, [full("cs")])
 
@@ -209,27 +212,27 @@ def rank_program(g, core, T, topo):
     iota("cm", 0, NL, [[0, 12], [1, 16]], 0, 0, **small)
     for t in range(3):
         iota("pb%d" % t, 0, NL, [[1, NL]], 1344 + NL * t, 0, **small)
+    iota("w0", 0, WW, [[0, WW]], 0, 0, **small)
     V([("pci", 0, 1)], [("pci", 1, 2)], v1(T.pci[:, 1:2], T.pci[:, 0:1], 15, A.bitwise_and))
     V([("pci", 0, 1)], [("pci", 2, 3)], v1(T.pci[:, 2:3], T.pci[:, 0:1], 4, A.logical_shift_right))
     fill("sel16", 0, 2048, 0.0)
     V([("pci", 1, 3)], [("pcf", 1, 3)], vc(T.pcf[:, 1:3], T.pci[:, 1:3]))
     copy(col("tu0"), col("lt"))
-    copy(col("tt", 0, 8), col("cs", 0, 8)) if False else copy(col("csf", 0, 8), col("cs", 0, 8))
+    copy(col("csf", 0, 3), col("cs", 0, 3))
     V([full("cd"), ("pcf", 2, 3)], [full("bo")], v1(T.bo[:], T.cd[:], T.pcf[:, 2:3], A.is_equal))
-    V([full("csf")], [full("nsl")], v1(T.nsl[:], T.csf[:], -1.0, A.mult))
+    V([("csf", 0, 3)], [("nsl", 0, 3)], v1(T.nsl[:, 0:3], T.csf[:, 0:3], -1.0, A.mult))
     V([("pcf", 1, 2)], [("pcf", 3, 4)], v1(T.pcf[:, 3:4], T.pcf[:, 1:2], float(W), A.add))
     for t in range(3):
         V([("pcf", 1, 2)], [("pcf", 4 + t, 5 + t)], v1(T.pcf[:, 4 + t:5 + t], T.pcf[:, 1:2], float(t), A.is_equal))
     for k in range(16):
-        V([full("bo")], [("sel16", 128 * k, 128 * k + 128)], vc(T.sel16[:, 128 * k + k:128 * k + 128:16], T.bo[:, 0:128:16]))
+        S([full("bo")], [("sel16", 128 * k, 128 * k + 128)],
+          lambda k=k: s.activation(T.sel16[:, 128 * k + k:128 * k + 128:16], T.bo[:, 0:128:16], AF.Copy))
     copy(col("a0u"), col(("pk", 1344)))
 
     def more_constants():
         V([full("bo")], [full("nb")], v1(T.nb[:], T.bo[:], -17.0, A.mult))
         fill("rm", 0, E, 1.0)
-        V([full("bo"), full("csf")], [full("wth")], v1(T.wth[:], T.bo[:], T.csf[:, 4:5], A.mult))
         V([full("rm")], [full("rm")], lambda: v.memset(T.rm[:, 0:E:16], 0.0))
-        fill("w0", 0, WW, 0.0)
 
     def second_package():
         V([full("pvi")], [full("pvo")], vc(T.pvo[:, 0:24:2], T.pvi[:]))
@@ -240,7 +243,7 @@ def rank_program(g, core, T, topo):
     ODD, EVEN = 1, 0
     BANK_OF = [0, 1, 0, 1, 0, 1]
 
-    def step1(tab, low, tu, tn, a0u, a0n, a1u, a1n, bias, q, t2u, filler):
+    def step1(tab, low, tu, tn, a0u, a0n, a1u, a1n, bias, q, t2u, filler, claims=None):
         def lanes(x, j):
             return col(x, CUTS[j], CUTS[j + 1])
 
@@ -249,7 +252,7 @@ def rank_program(g, core, T, topo):
 
         def xg(tr, lst, j):
             l, o = lanes(lst, j), items("xs%d" % tr, j)
-            S([full(tab), l[1], full(bias[0])], [o[1]],
+            S([full(tab), l[1], (bias[0], bias[1], bias[1] + 1)], [o[1]],
               lambda: s.activation(o[0], T[tab][:, 0:W].indirect(l[0]), AF.Identity, bias=T[bias[0]][:, bias[1]:bias[1] + 1]))
 
         def compare(tr, lst, j):
@@ -274,13 +277,15 @@ def rank_program(g, core, T, topo):
                 a, d = lanes(a1n, j), lanes((out, EVEN, 2), j)
                 V([a[1], ro], [ro], vt(d[0], a[0], new[0], A.subtract))
 
-        def x2g(j):
-            l, o = lanes(t2u, j), items("x2", j)
-            kw = {} if low else {"scale": -1.0, "bias": 255.0}
-            S([full(tab), l[1]], [o[1]], lambda: s.activation(o[0], T[tab][:, 0:W].indirect(l[0]), AF.Identity, **kw))
+        def rows(j):
+            if claims is not None:
+                claim_rows(claims, (q, ODD, 2), CUTS[j], CUTS[j + 1])
 
         for j in range(3):
             xg(0, tu, j)
+        if not low:
+            plain(6)
+            plain(7)
         t, a = col(tn), col(a0n)
         V([t[1]], [("at", 1, 384)], vc(T.at[:, 1:384:2], t[0]))
         V([a[1], t[1]], [("at", 0, 383)], vt(T.at[:, 0:383:2], a[0], t[0], A.subtract))
@@ -298,16 +303,20 @@ def rank_program(g, core, T, topo):
         xg(1, "t1u", 2)
         compare(1, a1u, 1)
         choose(1, 0)
-        x2g(0)
+        final_x(tab, low, t2u, 0)
+        rows(0)
         compare(1, a1u, 2)
         choose(1, 1)
-        x2g(1)
+        final_x(tab, low, t2u, 1)
+        rows(1)
         filler[2]()
         choose(1, 2)
+        rows(2)
+        final_x(tab, low, t2u, 2)
 
-    def last_x2(tab, low, t2u):
-        kw = {} if low else {"scale": -1.0, "bias": 255.0}
-        l, o = col(t2u, CUTS[2], NL), col("x2", 16 * CUTS[2], E)
+    def final_x(tab, low, t2u, j):
+        kw = {} if low else {"scale": -1.0, "bias": MAGIC + 255.0}
+        l, o = col(t2u, CUTS[j], CUTS[j + 1]), col("x2", 16 * CUTS[j], 16 * CUTS[j + 1])
         S([full(tab), l[1]], [o[1]], lambda: s.activation(o[0], T[tab][:, 0:W].indirect(l[0]), AF.Identity, **kw))
 
     def scan(j):
@@ -334,10 +343,12 @@ def rank_program(g, core, T, topo):
                 lambda: V([full("sm")], [full("tn")], v1(T.tn[:], T.sm[:], 4095, A.bitwise_and)),
                 lambda: V([full("tn")], [o[1]], vc(o[0], T.tn[:]))]
 
-    def bound():
+    def bound_sums():
         run("p", [full("mk0"), full("mk1"), full("bo"), full("nb")], [("cn1", 0, NL)],
             lambda: te.matmul(T.cn1[:, 0:NL], T.bo[:], T.mk0[:, 1:384:2], True, False),
             lambda: te.matmul(T.cn1[:, 0:NL], T.nb[:], T.mk1[:, 1:384:2], False, True))
+
+    def bound_sel():
         V([("cn1", 0, NL)], [full("sel")], v1(T.sel[:], T.cn1[:, 0:NL], 0.5, A.is_ge))
 
     def pick(first, second, out, c0):
@@ -346,20 +357,17 @@ def rank_program(g, core, T, topo):
                 lambda: V([d[1], full("sel")], [d[1]], vt(d[0], d[0], T.sel[:], A.mult)),
                 lambda: V([d[1], z[1]], [o[1]], vt(o[0], d[0], z[0], A.add))]
 
-    def claim_ones():
-        run("p", [full("onef")], [("cn0", 0, NL)], lambda: te.matmul(T.cn0[:, 0:NL], T.onef[0:1, 0:128], T.onef[0:1, 0:NL], True, False))
-
-    def claim_rows(t, t2):
-        x = col(t2)
-        run("p", [x[1], full("ts"), full("onef")], [("cn0", 0, NL)],
-            lambda: te.matmul(T.cn0[:, 0:NL], T.ts[:, 128 * t:128 * t + 128], x[0], False, True))
+    def claim_rows(t, t2, lo, hi):
+        x = col(t2, lo, hi)
+        run("p", [full("oneb")], [("vs", lo, hi)], lambda: te.matmul(T.vs[:, lo:hi], T.oneb[0:1, 0:128], T.oneb[0:1, 0:hi - lo], True, False))
+        run("p", [x[1], full("ts")], [("vs", lo, hi)], lambda: te.matmul(T.vs[:, lo:hi], T.ts[:, 128 * t:128 * t + 128], x[0], False, True))
 
     def claim_list(t):
         rm = ("rm", 0, NL)
         return [
-            lambda: V([("cn0", 0, NL), full("dm")], [full("cmk")], vt(T.cmk[:], T.cn0[:, 0:NL], T.dm[:], A.mult)),
+            lambda: V([("vs", 0, NL), full("dm")], [full("cmk")], vt(T.cmk[:], T.vs[:, 0:NL], T.dm[:], A.mult)),
             lambda: V([full("cmk"), rm], [full("cs1")], lambda: v.tensor_tensor_scan(T.cs1[:], T.rm[:, 0:NL], T.cmk[:], 0.0, A.mult, A.add)),
-            lambda: V([("cn0", 0, NL), full("cs1")], [full("cse")], vt(T.cse[:], T.cn0[:, 0:NL], T.cs1[:], A.is_equal)),
+            lambda: V([("vs", 0, NL), full("cs1")], [full("cse")], vt(T.cse[:], T.vs[:, 0:NL], T.cs1[:], A.is_equal)),
             lambda: V([full("cse"), rm], [full("cs2")], lambda: v.tensor_tensor_scan(T.cs2[:], T.rm[:, 0:NL], T.cse[:], 0.0, A.mult, A.add)),
             lambda: V([full("cs2")], [full("ct1")], v2(T.ct1[:], T.cs2[:, 15:NL:16], 8192.0, -8193.0, A.mult, A.add)),
             lambda: V([full("ct1"), full("cs1")], [full("ct2")], vt(T.ct2[:], T.ct1[:], T.cs1[:, 15:NL:16], A.add))] + (
@@ -377,25 +385,31 @@ def rank_program(g, core, T, topo):
             V([rg, full("of")], [(w, 0, WW)], vc(T[w][:, 0:WW].indirect(T.of[:, 2 * c:2 * c + 1]), src))
         return [lambda c=c: call(c) for c in range(12)]
 
-    def floor_const(i):
-        db = "db%d" % (i % 5)
-        run("p", [full("cstb"), full("oneb")], [(db, 0, 512)], lambda: te.matmul(T[db][:], T.cstb[0:1, :], T.oneb[0:1, :], True, False))
+    def bank(i):
+        return ["db0", "db1", "db2", "db3", "db4", "cn0", "cn1", "vs"][i]
 
-    def sums(t, i):
-        db, w = "db%d" % (i % 5), "w%d" % t
-        run("p", [(w, 0, WW), full("qm")], [(db, 0, 512)],
-            lambda: te.matmul(T[db][:], T.qm[:], T[w][:, 512 * i:512 * i + 512], False, True))
+    def before(t, i, parts=(0, 1)):
+        db, lo, hi = bank(i), 512 * i, 512 * i + 512
+        k = 2 if t == 0 else 1
+        cs, (m, b) = ("cst2" if t == 0 else "cstb"), (("nid", "pl") if t == 0 else ("idm", "c"))
+        if 0 in parts:
+            run("p", [full(cs), full("oneb")], [(db, 0, 512)], lambda: te.matmul(T[db][:], T[cs][0:k, :], T.oneb[0:k, :], True, False))
+        if 1 in parts:
+            run("p", [(b, lo, hi), full(m)], [(db, 0, 512)], lambda: te.matmul(T[db][:], T[m][:], T[b][:, lo:hi], False, False))
 
-    def rise(t, i):
-        db, lo, hi = "db%d" % (i % 5), 512 * i, 512 * i + 512
-        V([(db, 0, 512), ("u", lo, hi)], [("u", lo, hi)], vt(T.u[:, lo:hi], T[db][:], T.u[:, lo:hi], A.add))
-        S([("u", lo, hi)], [("c", lo, hi)], lambda: s.activation(T.c[:, lo:hi], T.u[:, lo:hi], AF.Relu, bias=MAGIC + 255.0, scale=-1.0))
-        if i < 3:
-            floor_const(i + 5)
-            sums(t, i + 5)
+    def sums(t):
+        for i in range(8):
+            db, w = bank(i), "w%d" % t
+            run("p", [(w, 0, WW), full("qm")], [(db, 0, 512)],
+                lambda: te.matmul(T[db][:], T.qm[:], T[w][:, 512 * i:512 * i + 512], False, True))
 
-    def nothing():
-        pass
+    def rise(i):
+        db, lo, hi = bank(i), 512 * i, 512 * i + 512
+        V([(db, 0, 512)], [("dd", lo, hi)], v2(T.dd[:, lo:hi], T[db][:], 0.0, MAGIC, A.max, A.add))
+
+    def plain(i):
+        lo, hi = 512 * i, 512 * i + 512
+        S([("dd", lo, hi)], [("c", lo, hi)], lambda: s.activation(T.c[:, lo:hi], T.dd[:, lo:hi], AF.Identity, bias=-MAGIC))
 
     send_wide("pri")
     send("cst")
@@ -403,17 +417,19 @@ def rank_program(g, core, T, topo):
           [more_constants, second_package, lambda: scan(0)])
     stage("t2", T.t2u0, [full("t2u0")])
     send("t2")
-    last_x2("ph", True, "t2u0")
     shifted(0, "q0")
     lots_of("q0")
     take("y", "cst", T.cso[:], [full("cso")])
     take("y", "t2", T.o2u[:], [full("o2u")])
     dma("y", T.yh[:, 0:NL], T.tf[:], [full("tf")], [])
-    bound()
+    bound_sums()
+    bound_sel()
     weave(pick(("pk", 1344), "a1f", "b1f", 0), pick("pb0", "pnr", "par0", NL))
     copy(col(("m4u", NL)), col("b1f"))
     copy(col(("m4u", 2 * NL)), col("par0"))
+    copy(col("csf", 3, 8), col("cs", 3, 8))
     scan(1)
+    V([full("bo"), ("csf", 3, 8)], [full("wth")], v1(T.wth[:], T.bo[:], T.csf[:, 4:5], A.mult))
     scan(2)
     weigh("wth")
 
@@ -432,48 +448,44 @@ def rank_program(g, core, T, topo):
     def c_ts(t):
         V([full("bo"), ("pcf", 4 + t, 5 + t)], [("ts", 128 * t, 128 * t + 128)],
           v1(T.ts[:, 128 * t:128 * t + 128], T.bo[:], T.pcf[:, 4 + t:5 + t], A.mult))
-    weave([lambda: c_eq(), lambda: fill("onef", 0, NL, 1.0), lambda: c_id(), lambda: c_ts(0), lambda: c_qk(), lambda: c_dm(),
-           lambda: fill("cstb", 0, 128, -63.0 / 128.0), lambda: fill("oneb", 0, 512, 1.0)], next_lots("q0", ("m4u", 0)))
+    weave([c_eq, c_dm, c_id, lambda: c_ts(0), c_qk, lambda: fill("cstb", 0, 128, 63.0 / 128.0), lambda: fill("oneb", 0, 512, 1.0)],
+          next_lots("q0", ("m4u", 0)))
     stage("m4", T.m4u, [full("m4u")])
     send("m4")
     for w in ("w1", "w2"):
         iota(w, 0, WW, [[0, WW]], 0, 0, **small)
-    take("s", "pri", T.pl[:], [full("pl")])
-    claim_ones()
+    take("s", "pri", T.pl[:, 0:W], [("pl", 0, W)])
     copy(col("cof", 0, 8), col("cso", 0, 8))
-    fill("u", W, WW, MAGIC)
-    V([full("idm"), full("cof")], [full("dg")], v2(T.dg[:], T.idm[:], T.cof[:, 3:4], 1.0 / 64.0, A.mult, A.mult))
+    fill("pl", W, WW, 0.0)
+    V([full("idm"), full("cof")], [full("dg")], v2(T.dg[:], T.idm[:], T.cof[:, 3:4], -1.0 / 64.0, A.mult, A.mult))
     run("p", [full("qk"), full("dg")], [("cn1", 0, 128)], lambda: te.matmul(T.cn1[:, 0:128], T.qk[:], T.dg[:], True, True))
+    V([full("idm")], [full("nid")], v1(T.nid[:], T.idm[:], -1.0, A.mult))
+    fill("cst2", 0, 128, 63.0 / 128.0)
+    V([], [full("cst2")], lambda: v.memset(T.cst2[0:1, :], 255.0))
     c_ts(1)
     c_ts(2)
     V([full("bo"), full("cof")], [full("wto")], v1(T.wto[:], T.bo[:], T.cof[:, 4:5], A.mult))
     V([("cn1", 0, 128)], [full("qm")], vc(T.qm[:], T.cn1[:, 0:128]))
-    for i in range(5):
-        floor_const(i)
-    for h in range(2):
-        (o, ro), (p, rp) = col("u", 2048 * h, 2048 * h + 2048), col("pl", 2048 * h, 2048 * h + 2048)
-        S([rp], [ro], lambda o=o, p=p: s.activation(o, p, AF.Identity, bias=MAGIC))
+    for i in range(7):
+        before(0, i, (0,))
     copy(col("o2f"), col("o2u"))
-    claim_rows(0, "o2f")
+    claim_rows(0, "o2f", 0, NL)
     weave(claim_list(0))
-    S([("u", 0, WW), full("vl")], [full("v0")], lambda: s.activation(T.v0[:], T.u[:, 0:WW].indirect(T.vl[:, 0:12]), AF.Identity, bias=-MAGIC))
+    S([("pl", 0, WW), full("vl")], [full("v0")], lambda: s.activation(T.v0[:], T.pl[:, 0:WW].indirect(T.vl[:, 0:12]), AF.Identity))
+    for i in range(8):
+        before(0, i, (1,) if i < 7 else (0, 1))
     weave(scatter(0))
     take("y", "m4", T.mo[:], [full("mo")])
-    for i in range(5):
-        sums(0, i)
+    sums(0)
     for i in range(8):
-        rise(0, i)
+        rise(i)
+        if i < 6:
+            plain(i)
     copy(col("mof", 0, 384), col(("mo", NL), 0, 384))
     dma("y", T.yv[:, 0:NL], T.par0[0:128:16, :], [full("par0")], [])
     for i in range(5):
-        floor_const(i)
-
-    def scan_first():
-        scan(0)
-        claim_ones()
-    step1("c", False, "mo", "mo", "o2u", "o2f", ("mo", NL), "mof", ("cof", 1), "q1", "t2u1", [nothing, nothing, scan_first])
-    claim_rows(1, ("q1", ODD, 2))
-    last_x2("c", False, "t2u1")
+        before(1, i)
+    step1("dd", False, "mo", "mo", "o2u", "o2f", ("mo", NL), "mof", ("cof", 1), "q1", "t2u1", [nothing, nothing, lambda: scan(0)], 1)
     shifted(1, "q1")
     lots_of("q1")
     stage("y1", T.tf, [full("tf")])
@@ -484,48 +496,56 @@ def rank_program(g, core, T, topo):
     scan(2)
     weigh("wto")
     weave(cl[4:])
+    before(1, 5)
     weave(scatter(1), [nothing, nothing] + next_lots("q1", "tnu"))
-    for i in range(5):
-        sums(1, i)
+    before(1, 6)
+    before(1, 7)
+    sums(1)
     for i in range(8):
-        rise(1, i)
-    bound()
+        rise(i)
+        if i < 6:
+            plain(i)
+    bound_sums()
+    bound_sel()
     weave(pick("o2f", "mof", "b1f", 0), pick("pb1", ("mof", NL), "par12", NL))
     copy(col("b1u"), col("b1f"))
     take("y", "y1", T.yh[:, NL:2 * NL], [])
     for i in range(5):
-        floor_const(i)
-    step1("c", False, "tnu", "tn", "t2u1", ("q1", ODD, 2), "b1u", "b1f", ("cof", 2), "q2", "t2u2", [nothing, nothing, claim_ones])
-    claim_rows(2, ("q2", ODD, 2))
-    last_x2("c", False, "t2u2")
+        before(2, i)
+    step1("dd", False, "tnu", "tn", "t2u1", ("q1", ODD, 2), "b1u", "b1f", ("cof", 2), "q2", "t2u2", [nothing, nothing, nothing], 2)
     lots_of("q2")
     stage("y2", T.tf, [full("tf")])
     send("y2")
-    bound()
-    weave(pick("pb2", "par12", ("par12", NL), 0))
+    bound_sums()
+    weave(claim_list(2))
+    before(2, 5)
+    weave(scatter(2), [nothing, bound_sel] + pick("pb2", "par12", ("par12", NL), 0))
+    before(2, 6)
+    before(2, 7)
     stage("par", T.par12, [full("par12")], rows=True)
     send("par")
-    weave(claim_list(2))
-    weave(scatter(2))
-    for i in range(5):
-        sums(2, i)
+    sums(2)
+
+    def price(i):
+        lo, hi = 512 * i, 512 * i + 512
+        if i < 7:
+            S([("dd", lo, hi)], [("pf", lo, hi)], lambda: s.activation(T.pf[:, lo:hi], T.dd[:, lo:hi], AF.Identity, scale=-1.0, bias=MAGIC + 255.0))
+        else:
+            V([("dd", lo, hi)], [("pf", lo, hi)], v2(T.pf[:, lo:hi], T.dd[:, lo:hi], -1.0, MAGIC + 255.0, A.mult, A.add))
 
     def ship(b):
-        (c, rc), (p, rp) = col("c", BLOCKS[b], BLOCKS[b + 1]), col("pf", BLOCKS[b], BLOCKS[b + 1])
-        V([rc], [rp], v2(p, c, -1.0, 255.0, A.mult, A.add))
+        p, rp = col("pf", BLOCKS[b], BLOCKS[b + 1])
         m = "o%d" % b
         dma("y", T["s_" + m][:], p, [rp], [full("s_" + m)])
         dma("y", T["l_" + m][rank], T.pf[mine, BLOCKS[b]:BLOCKS[b + 1]], [rp], [full("l_" + m)])
         send(m)
     nxt = 0
     for i in range(8):
-        rise(2, i)
-        if nxt < NB - 1 and BLOCKS[nxt + 1] <= 512 * i:
+        rise(i)
+        price(i)
+        if BLOCKS[nxt + 1] <= 512 * i + 512:
             ship(nxt)
             nxt += 1
-    while nxt < NB:
-        ship(nxt)
-        nxt += 1
     take("s", "y2", T.yh[:, 2 * NL:3 * NL], [])
     take("s", "par", T.yv[:, NL:3 * NL], [])
     for b in range(NB):

import numpy as np
from concourse.bass import DstId, RemoteDMATransfer
from concourse.mybir import dt, AluOpType, AxisListType, ActivationFunctionType

A = AluOpType
AF = ActivationFunctionType
MAGIC = 12582912.0
NL = 192
E = 16 * NL
W = 4096
WW = W + 16
CUTS = [0, 64, 128, 192]
BLOCKS = [0, 1024, 2048, 3072, 3584, W]
NB = len(BLOCKS) - 1
SCRATCH = {}
for _d, _n, _names in (
        ("bfloat16", W, "ph c pf"), ("bfloat16", WW, "w0 w1 w2 pl"), ("float32", W, "dd"), ("int32", 1536, "pk"),
        ("int32", NL, "lt pnr ui uj pr ps sm tn"), ("int32", 12, "pvi"), ("uint16", 24, "pvo of"), ("uint16", 12, "vl"),
        ("int32", 8, "cs cso pci"), ("float32", 8, "csf nsl cof pcf"), ("float32", 128, "cd"), ("float32", 384, "ts par12 at tt q0 q1 q2"),
        ("bfloat16", 128, "bo nb eq idm nid qk dg qm wth wto cstb cst2"), ("bfloat16", 512, "oneb"), ("bfloat16", 2048, "sel16"),
        ("bfloat16", E, "rm ind x2 sc"), ("float32", E, "xs0 xs1"), ("bfloat16", NL, "cse v0"), ("bfloat16", 384, "mk0 mk1"),
        ("float32", NL, "cm dm pb0 pb1 pb2 a1f sel tf o2f par0 b1f tc cmk cs1 cs2"),
        ("uint16", NL, "tu0 a0u a1u t1u t2u0 t2u1 t2u2 o2u b1u tnu"), ("float32", 12, "ct1 ct2"),
        ("uint16", 576, "m4u mo"), ("float32", 384, "mof")):
    for _k in _names.split():
        SCRATCH[_k] = ("sbuf", [128, _n], _d)
MSG = []
for _k, _n, _d in [("cst", 1, "int32"), ("pri", 512, "bfloat16"), ("t2", 24, "uint16"), ("m4", 72, "uint16"), ("y1", 24, "float32"),
                   ("y2", 24, "float32"), ("par", 3, "float32")] + [("o%d" % _b, (BLOCKS[_b + 1] - BLOCKS[_b]) // 8, "bfloat16") for _b in range(NB)]:
    MSG.append(_k)
    SCRATCH["s_" + _k] = SCRATCH["l_" + _k] = ("dram", [8, 128, _n], _d)
BANKS = ["cn0", "cn1", "vs", "db0", "db1", "db2", "db3", "db4"]
for _k in BANKS:
    SCRATCH[_k] = ("psum", [128, 512], "float32")
SEMAPHORES = ["vv", "ss", "pe", "gg", "lsem"] + ["d%d" % _i for _i in range(64)] + ["ar_" + _m for _m in MSG]


def rank_program(g, core, T, topo):
    rank = T.rank_of(core)
    if rank is None:
        return
    cores = [int(c) for c in T.cores]
    N = len(cores)

    eng = {"v": g.vector, "s": g.scalar, "p": g.tensor, "g": g, "y": g.sync}
    sem_of = {"v": "vv", "s": "ss", "p": "pe", "g": "gg"}
    count = {"vv": 0, "ss": 0, "pe": 0, "gg": 0, "d": 0}
    know = {q: {} for q in eng}
    snap = {}
    hist = {}
    total = {}
    seen = {}

    def wait(q, sem, val):
        if know[q].get(sem, 0) >= val:
            return
        eng[q].wait_ge(T.sem[sem], val)
        seen[sem] = max(seen.get(sem, 0), val)
        know[q][sem] = val
        for k, n in snap.get((sem, val), {}).items():
            know[q][k] = max(know[q].get(k, 0), n)

    def settle(q, reads, writes, is_dma):
        for (b, lo, hi), wr in [(r, False) for r in reads] + [(w, True) for w in writes]:
            bank = b in BANKS
            for e in hist.get(b, []):
                over = e[0] < hi and lo < e[1]
                if e[2] == q and not is_dma:
                    need = over and (e[5] or (wr and bank))
                else:
                    need = bank or (over and (wr or e[5]))
                if need:
                    wait(q, e[3], e[4])

    def record(q, sem, val, reads, writes):
        for (b, lo, hi) in writes:
            hist[b] = [e for e in hist.get(b, []) if not (lo <= e[0] and e[1] <= hi)] + [(lo, hi, q, sem, val, True)]
        for (b, lo, hi) in reads:
            old = hist.get(b, [])
            hist[b] = [e for e in old if not (e[:3] == (lo, hi, q) and not e[5] and q != "d")] + [(lo, hi, q, sem, val, False)]

    def run(q, reads, writes, *fns):
        settle(q, reads, writes, False)
        for f in fns[:-1]:
            f()
        sem = sem_of[q]
        count[sem] += 1
        val = total[sem] = count[sem]
        fns[-1]().then_inc(T.sem[sem], 1)
        snap[(sem, val)] = dict(know[q])
        snap[(sem, val)][sem] = val
        record(q, sem, val, reads, writes)

    def dma(q, out, in_, reads, writes):
        settle(q, reads, writes, True)
        sem = "d%d" % count["d"]
        count["d"] += 1
        total[sem] = 16
        eng[q].dma_start(out, in_).then_inc(T.sem[sem], 16)
        snap[(sem, 16)] = dict(know[q])
        record("d", sem, 16, reads, writes)

    def full(name):
        return (name, 0, 1 << 20)

    def col(x, lo=0, hi=NL):
        if x in SCRATCH:
            x = (x, 0)
        b, st = x[0], x[2] if len(x) > 2 else 1
        i, j = x[1] + lo * st, x[1] + (hi - 1) * st + 1
        return (T[b][:, i:j] if st == 1 else T[b][:, i:j:st]), (b, i, j)

    def V(reads, writes, f):
        run("v", reads, writes, f)

    def S(reads, writes, f):
        run("s", reads, writes, f)

    v, s, te = g.vector, g.scalar, g.tensor

    def vt(out, in0, in1, op):
        return lambda: v.tensor_tensor(out, in0, in1, op)

    def vc(out, in_):
        return lambda: v.tensor_copy(out, in_)

    def v1(out, in0, s1, op):
        return lambda: v.tensor_scalar(out, in0, s1, None, op)

    def v2(out, in0, s1, s2, op0, op1):
        return lambda: v.tensor_scalar(out, in0, s1, s2, op0, op1)

    def copy(out, in_):
        V([in_[1]], [out[1]], vc(out[0], in_[0]))

    def fill(b, lo, hi, x):
        V([], [(b, lo, hi)], lambda: v.memset(T[b][:, lo:hi], x))

    def weave(*chains):
        for i in range(max(len(c) for c in chains)):
            for c in chains:
                if i < len(c):
                    c[i]()

    def nothing():
        pass

    others = [(rank + j) % N for j in range(1, N)]
    away = [d for d in others if topo.chip(cores[d]) != topo.chip(core)]
    near = [d for d in others if topo.chip(cores[d]) == topo.chip(core)]
    offe = topo.engines(core, cores[away[0]])
    one = [e for e in topo.engines(core, cores[near[0]]) if e not in offe]
    turn = [0]
    arrive = {m: 0 for m in MSG}

    def fused(m, plan):
        settle("g", [full("s_" + m)], [], True)
        tr = []
        for d, es in plan:
            rid, pid, _e = topo.addr(cores[d])
            tr.append(RemoteDMATransfer(dst_ids=[DstId(rid=rid, pnc=pid)], dma_engine_mask=sum(1 << e for e in es),
                                        remote_sem=T.sem["ar_" + m], src=T["s_" + m][d], dst=T["l_" + m][rank]))
        g.remote_dma_fused(tr, local_sem=T.sem.lsem)
        n = sum(len(es) for d, es in plan)
        total["lsem"] = total.get("lsem", 0) + n
        arrive[m] += n

    def send(m):
        plan = [(d, [offe[(turn[0] + j) % len(offe)]]) for j, d in enumerate(away)]
        turn[0] += len(away)
        fused(m, plan + [(d, one[0:3:2]) for d in near])

    def send_wide(m):
        fused(m, [(d, offe[2 * j:2 * j + 2]) for j, d in enumerate(away[:4])] + [(d, one[0:3:2]) for d in near])
        fused(m, [(d, offe[4 * j:4 * j + 4]) for j, d in enumerate(away[4:])])

    def landed(q, m):
        total["ar_" + m] = arrive[m]
        wait(q, "ar_" + m, arrive[m])

    mine = slice(16 * rank, 16 * rank + 16)

    def stage(m, in_, reads, rows=None):
        dma("y", T["s_" + m][:], in_[:] if rows is None else in_[0:128:16, :], reads, [full("s_" + m)])
        dma("y", T["l_" + m][rank], in_[mine, :] if rows is None else in_[16 * rank:16 * rank + 1, :], reads, [full("l_" + m)])

    def take(q, m, out, writes):
        landed(q, m)
        dma(q, out, T["l_" + m][:], [full("l_" + m)], writes)

    fill("cs", 0, 8, 0)
    fill("pnr", 0, NL, 0)
    fill("mk0", 0, 384, 0.0)
    fill("mk1", 0, 384, 0.0)
    dma("s", T.lt[:], T.lots[:], [], [full("lt")])
    dma("y", T.cs[:, 0:3], T.slack[:], [], [("cs", 0, 3)])
    dma("y", T.ph[:], T.price[:], [], [full("ph")])
    dma("s", T.pk[:, 1344:1536], T.packs[:, 1344:1536], [], [("pk", 1344, 1536)])
    dma("s", T.pvi[:], T.prev[:, 1344:1536], [], [full("pvi")])
    dma("y", T.pk[:, 0:1344], T.packs[:, 0:1344], [], [("pk", 0, 1344)])
    dma("s", T.cs[:, 3:4], T.inc[:], [], [("cs", 3, 4)])
    dma("s", T.cs[:, 4:5], T.wt[:], [], [("cs", 4, 5)])
    dma("s", T.pnr[0:128:16, :], T.prev[:, 1344:1536], [], [full("pnr")])
    stage("pri", T.price, [])
    stage("cst", T.cs, [full("cs")])

    def iota(b, lo, hi, pat, base, cm, **kw):
        run("g", [], [(b, lo, hi)], lambda: g.iota(T[b][:, lo:hi], pat, base, cm, **kw))
    small = {"allow_small_or_imprecise_dtypes": True}
    iota("pci", 0, 1, [[0, 1]], 0, 1)
    iota("cd", 0, 128, [[1, 8], [0, 16]], 0, 0, **small)
    iota("cm", 0, NL, [[0, 12], [1, 16]], 0, 0, **small)
    for t in range(3):
        iota("pb%d" % t, 0, NL, [[1, NL]], 1344 + NL * t, 0, **small)
    iota("w0", 0, WW, [[0, WW]], 0, 0, **small)
    V([("pci", 0, 1)], [("pci", 1, 2)], v1(T.pci[:, 1:2], T.pci[:, 0:1], 15, A.bitwise_and))
    V([("pci", 0, 1)], [("pci", 2, 3)], v1(T.pci[:, 2:3], T.pci[:, 0:1], 4, A.logical_shift_right))
    fill("sel16", 0, 2048, 0.0)
    V([("pci", 1, 3)], [("pcf", 1, 3)], vc(T.pcf[:, 1:3], T.pci[:, 1:3]))
    copy(col("tu0"), col("lt"))
    copy(col("csf", 0, 3), col("cs", 0, 3))
    V([full("cd"), ("pcf", 2, 3)], [full("bo")], v1(T.bo[:], T.cd[:], T.pcf[:, 2:3], A.is_equal))
    V([("csf", 0, 3)], [("nsl", 0, 3)], v1(T.nsl[:, 0:3], T.csf[:, 0:3], -1.0, A.mult))
    V([("pcf", 1, 2)], [("pcf", 3, 4)], v1(T.pcf[:, 3:4], T.pcf[:, 1:2], float(W), A.add))
    for t in range(3):
        V([("pcf", 1, 2)], [("pcf", 4 + t, 5 + t)], v1(T.pcf[:, 4 + t:5 + t], T.pcf[:, 1:2], float(t), A.is_equal))
    for k in range(16):
        S([full("bo")], [("sel16", 128 * k, 128 * k + 128)],
          lambda k=k: s.activation(T.sel16[:, 128 * k + k:128 * k + 128:16], T.bo[:, 0:128:16], AF.Copy))
    copy(col("a0u"), col(("pk", 1344)))

    def more_constants():
        V([full("bo")], [full("nb")], v1(T.nb[:], T.bo[:], -17.0, A.mult))
        fill("rm", 0, E, 1.0)
        V([full("rm")], [full("rm")], lambda: v.memset(T.rm[:, 0:E:16], 0.0))

    def second_package():
        V([full("pvi")], [full("pvo")], vc(T.pvo[:, 0:24:2], T.pvi[:]))
        for c in range(12):
            V([full("pvo"), full("pk")], [("a1f", c, c + 1)], vc(T.a1f[:, c:NL:12], T.pk[:, 0:1536].indirect(T.pvo[:, 2 * c:2 * c + 1])))
        V([full("a1f")], [full("a1u")], vc(T.a1u[:], T.a1f[:]))

    ODD, EVEN = 1, 0
    BANK_OF = [0, 1, 0, 1, 0, 1]

    def step1(tab, low, tu, tn, a0u, a0n, a1u, a1n, bias, q, t2u, filler, claims=None):
        def lanes(x, j):
            return col(x, CUTS[j], CUTS[j + 1])

        def items(b, j):
            return col(b, 16 * CUTS[j], 16 * CUTS[j + 1])

        def xg(tr, lst, j):
            l, o = lanes(lst, j), items("xs%d" % tr, j)
            S([full(tab), l[1], (bias[0], bias[1], bias[1] + 1)], [o[1]],
              lambda: s.activation(o[0], T[tab][:, 0:W].indirect(l[0]), AF.Identity, bias=T[bias[0]][:, bias[1]:bias[1] + 1]))

        def compare(tr, lst, j):
            l, x, o, n = lanes(lst, j), items("xs%d" % tr, j), items("ind", j), CUTS[j + 1] - CUTS[j]
            V([full(tab), l[1], x[1]], [o[1]], vt(o[0], T[tab][:, 0:W].indirect(l[0]), x[0], A.is_lt if low else A.is_gt))
            cn = "cn%d" % BANK_OF[tr * 3 + j]
            run("p", [o[1], full("sel16")], [(cn, 0, n)],
                *[(lambda k=k: te.matmul(T[cn][:, 0:n], T.sel16[:, 128 * k:128 * k + 128], T.ind[:, o[1][1] + k:o[1][2]:16],
                                         k == 0, k == 15)) for k in range(16)])

        def choose(tr, j):
            n = CUTS[j + 1] - CUTS[j]
            cn, mk = "cn%d" % BANK_OF[tr * 3 + j], "mk%d" % tr
            src, out, lst = ("at", "tt", "t1u") if tr == 0 else ("tt", q, t2u)
            m, u = lanes((mk, ODD, 2), j), lanes(lst, j)
            (k, rk), (i, ri), (o, ro) = [col(b, 2 * CUTS[j], 2 * CUTS[j + 1]) for b in (mk, src, out)]
            new = lanes((out, ODD, 2), j)
            V([(cn, 0, n)], [m[1]], v1(m[0], T[cn][:, 0:n], 8.5, A.is_ge))
            V([rk, ri], [ro], lambda: v.tensor_tensor_scan(o, k, i, 0.0, A.mult, A.add))
            copy(u, new)
            if tr == 0:
                a, d = lanes(a1n, j), lanes((out, EVEN, 2), j)
                V([a[1], ro], [ro], vt(d[0], a[0], new[0], A.subtract))

        def rows(j):
            if claims is not None:
                claim_rows(claims, (q, ODD, 2), CUTS[j], CUTS[j + 1])

        for j in range(3):
            xg(0, tu, j)
        if not low:
            plain(6)
            plain(7)
        t, a = col(tn), col(a0n)
        V([t[1]], [("at", 1, 384)], vc(T.at[:, 1:384:2], t[0]))
        V([a[1], t[1]], [("at", 0, 383)], vt(T.at[:, 0:383:2], a[0], t[0], A.subtract))
        filler[0]()
        compare(0, a0u, 0)
        filler[1]()
        compare(0, a0u, 1)
        choose(0, 0)
        xg(1, "t1u", 0)
        compare(0, a0u, 2)
        choose(0, 1)
        xg(1, "t1u", 1)
        compare(1, a1u, 0)
        choose(0, 2)
        xg(1, "t1u", 2)
        compare(1, a1u, 1)
        choose(1, 0)
        final_x(tab, low, t2u, 0)
        rows(0)
        compare(1, a1u, 2)
        choose(1, 1)
        final_x(tab, low, t2u, 1)
        rows(1)
        filler[2]()
        choose(1, 2)
        rows(2)
        final_x(tab, low, t2u, 2)

    def final_x(tab, low, t2u, j):
        kw = {} if low else {"scale": -1.0, "bias": MAGIC + 255.0}
        l, o = col(t2u, CUTS[j], CUTS[j + 1]), col("x2", 16 * CUTS[j], 16 * CUTS[j + 1])
        S([full(tab), l[1]], [o[1]], lambda: s.activation(o[0], T[tab][:, 0:W].indirect(l[0]), AF.Identity, **kw))

    def scan(j):
        x, r, o = [col(b, 16 * CUTS[j], 16 * CUTS[j + 1]) for b in ("x2", "rm", "sc")]
        V([x[1], r[1]], [o[1]], lambda: v.tensor_tensor_scan(o[0], r[0], x[0], 0.0, A.mult, A.max))

    def lots_of(q):
        S([(q, 0, 384)], [full("tf")], lambda: s.activation(T.tf[:], T[q][:, 1:384:2], AF.Identity))

    def shifted(t, q):
        S([(q, 0, 384)], [full("tc")], lambda: s.activation(T.tc[:], T[q][:, 1:384:2], AF.Identity, bias=77.0 * (t + 1)))

    def weigh(wt):
        run("p", [full("sc"), full(wt)], [("cn1", 0, NL)], lambda: te.matmul(T.cn1[:, 0:NL], T[wt][:], T.sc[:, 15:E:16], True, True))

    def next_lots(q, tnu):
        o, w, t2 = col(tnu), col("vs"), col((q, ODD, 2))
        return [lambda: V([("cn1", 0, NL)], [full("ui")], vc(T.ui[:], T.cn1[:, 0:NL])),
                lambda: V([full("ui")], [full("uj")], v1(T.uj[:], T.ui[:], 1023, A.bitwise_and)),
                lambda: V([full("uj")], [w[1]], v2(w[0], T.uj[:], 2.0, 1.0, A.mult, A.add)),
                lambda: V([w[1], t2[1]], [full("pr")], vt(T.pr[:], w[0], t2[0], A.mult)),
                lambda: V([full("pr")], [full("ps")], v1(T.ps[:], T.pr[:], 5, A.logical_shift_right)),
                lambda: V([full("ps"), full("tc")], [full("sm")], vt(T.sm[:], T.ps[:], T.tc[:], A.add)),
                lambda: V([full("sm")], [full("tn")], v1(T.tn[:], T.sm[:], 4095, A.bitwise_and)),
                lambda: V([full("tn")], [o[1]], vc(o[0], T.tn[:]))]

    def bound_sums():
        run("p", [full("mk0"), full("mk1"), full("bo"), full("nb")], [("cn1", 0, NL)],
            lambda: te.matmul(T.cn1[:, 0:NL], T.bo[:], T.mk0[:, 1:384:2], True, False),
            lambda: te.matmul(T.cn1[:, 0:NL], T.nb[:], T.mk1[:, 1:384:2], False, True))

    def bound_sel():
        V([("cn1", 0, NL)], [full("sel")], v1(T.sel[:], T.cn1[:, 0:NL], 0.5, A.is_ge))

    def pick(first, second, out, c0):
        f, z, o, d = col(first), col(second), col(out), col(("vs", c0))
        return [lambda: V([f[1], z[1]], [d[1]], vt(d[0], f[0], z[0], A.subtract)),
                lambda: V([d[1], full("sel")], [d[1]], vt(d[0], d[0], T.sel[:], A.mult)),
                lambda: V([d[1], z[1]], [o[1]], vt(o[0], d[0], z[0], A.add))]

    def claim_rows(t, t2, lo, hi):
        x = col(t2, lo, hi)
        run("p", [full("oneb")], [("vs", lo, hi)], lambda: te.matmul(T.vs[:, lo:hi], T.oneb[0:1, 0:128], T.oneb[0:1, 0:hi - lo], True, False))
        run("p", [x[1], full("ts")], [("vs", lo, hi)], lambda: te.matmul(T.vs[:, lo:hi], T.ts[:, 128 * t:128 * t + 128], x[0], False, True))

    def claim_list(t):
        rm = ("rm", 0, NL)
        return [
            lambda: V([("vs", 0, NL), full("dm")], [full("cmk")], vt(T.cmk[:], T.vs[:, 0:NL], T.dm[:], A.mult)),
            lambda: V([full("cmk"), rm], [full("cs1")], lambda: v.tensor_tensor_scan(T.cs1[:], T.rm[:, 0:NL], T.cmk[:], 0.0, A.mult, A.add)),
            lambda: V([("vs", 0, NL), full("cs1")], [full("cse")], vt(T.cse[:], T.vs[:, 0:NL], T.cs1[:], A.is_equal)),
            lambda: V([full("cse"), rm], [full("cs2")], lambda: v.tensor_tensor_scan(T.cs2[:], T.rm[:, 0:NL], T.cse[:], 0.0, A.mult, A.add)),
            lambda: V([full("cs2")], [full("ct1")], v2(T.ct1[:], T.cs2[:, 15:NL:16], 8192.0, -8193.0, A.mult, A.add)),
            lambda: V([full("ct1"), full("cs1")], [full("ct2")], vt(T.ct2[:], T.ct1[:], T.cs1[:, 15:NL:16], A.add))] + (
            [lambda: V([full("ct2"), full("pcf")], [full("vl")], v1(T.vl[:], T.ct2[:], T.pcf[:, 3:4], A.min))] if t == 0 else []) + [
            lambda: V([full("ct2"), full("pcf")], [full("of")], v1(T.of[:, 0:24:2], T.ct2[:], T.pcf[:, 3:4], A.min))]

    def scatter(t):
        w = "w%d" % t

        def call(c):
            if t == 0:
                src, rg = col("v0", 16 * c, 16 * c + 16)
            else:
                src, rg = T.x2[:, 256 * c + t:256 * c + 256:16], ("x2", 256 * c, 256 * c + 256)
            V([rg, full("of")], [(w, 0, WW)], vc(T[w][:, 0:WW].indirect(T.of[:, 2 * c:2 * c + 1]), src))
        return [lambda c=c: call(c) for c in range(12)]

    def bank(i):
        return ["db0", "db1", "db2", "db3", "db4", "cn0", "cn1", "vs"][i]

    def before(t, i, parts=(0, 1)):
        db, lo, hi = bank(i), 512 * i, 512 * i + 512
        k = 2 if t == 0 else 1
        cs, (m, b) = ("cst2" if t == 0 else "cstb"), (("nid", "pl") if t == 0 else ("idm", "c"))
        if 0 in parts:
            run("p", [full(cs), full("oneb")], [(db, 0, 512)], lambda: te.matmul(T[db][:], T[cs][0:k, :], T.oneb[0:k, :], True, False))
        if 1 in parts:
            run("p", [(b, lo, hi), full(m)], [(db, 0, 512)], lambda: te.matmul(T[db][:], T[m][:], T[b][:, lo:hi], False, False))

    def sums(t):
        for i in range(8):
            db, w = bank(i), "w%d" % t
            run("p", [(w, 0, WW), full("qm")], [(db, 0, 512)],
                lambda: te.matmul(T[db][:], T.qm[:], T[w][:, 512 * i:512 * i + 512], False, True))

    def rise(i):
        db, lo, hi = bank(i), 512 * i, 512 * i + 512
        V([(db, 0, 512)], [("dd", lo, hi)], v2(T.dd[:, lo:hi], T[db][:], 0.0, MAGIC, A.max, A.add))

    def plain(i):
        lo, hi = 512 * i, 512 * i + 512
        S([("dd", lo, hi)], [("c", lo, hi)], lambda: s.activation(T.c[:, lo:hi], T.dd[:, lo:hi], AF.Identity, bias=-MAGIC))

    send_wide("pri")
    send("cst")
    step1("ph", True, "tu0", "lt", "a0u", ("pk", 1344), "a1u", "a1f", ("nsl", 0), "q0", "t2u0",
          [more_constants, second_package, lambda: scan(0)])
    stage("t2", T.t2u0, [full("t2u0")])
    send("t2")
    shifted(0, "q0")
    lots_of("q0")
    take("y", "cst", T.cso[:], [full("cso")])
    take("y", "t2", T.o2u[:], [full("o2u")])
    dma("y", T.yh[:, 0:NL], T.tf[:], [full("tf")], [])
    bound_sums()
    bound_sel()
    weave(pick(("pk", 1344), "a1f", "b1f", 0), pick("pb0", "pnr", "par0", NL))
    copy(col(("m4u", NL)), col("b1f"))
    copy(col(("m4u", 2 * NL)), col("par0"))
    copy(col("csf", 3, 8), col("cs", 3, 8))
    scan(1)
    V([full("bo"), ("csf", 3, 8)], [full("wth")], v1(T.wth[:], T.bo[:], T.csf[:, 4:5], A.mult))
    scan(2)
    weigh("wth")

    def c_dm():
        V([("pcf", 1, 2), full("cm")], [full("dm")], v1(T.dm[:], T.cm[:], T.pcf[:, 1:2], A.is_equal))

    def c_eq():
        V([("pcf", 1, 2), full("cm")], [full("eq")], v1(T.eq[:], T.cm[:, 0:128], T.pcf[:, 1:2], A.is_equal))

    def c_id():
        V([full("eq"), full("bo")], [full("idm")], vt(T.idm[:], T.eq[:], T.bo[:], A.mult))

    def c_qk():
        V([full("eq"), full("idm")], [full("qk")], vt(T.qk[:], T.eq[:], T.idm[:], A.subtract))

    def c_ts(t):
        V([full("bo"), ("pcf", 4 + t, 5 + t)], [("ts", 128 * t, 128 * t + 128)],
          v1(T.ts[:, 128 * t:128 * t + 128], T.bo[:], T.pcf[:, 4 + t:5 + t], A.mult))
    weave([c_eq, c_dm, c_id, lambda: c_ts(0), c_qk, lambda: fill("cstb", 0, 128, 63.0 / 128.0), lambda: fill("oneb", 0, 512, 1.0)],
          next_lots("q0", ("m4u", 0)))
    stage("m4", T.m4u, [full("m4u")])
    send("m4")
    for w in ("w1", "w2"):
        iota(w, 0, WW, [[0, WW]], 0, 0, **small)
    take("s", "pri", T.pl[:, 0:W], [("pl", 0, W)])
    copy(col("cof", 0, 8), col("cso", 0, 8))
    fill("pl", W, WW, 0.0)
    V([full("idm"), full("cof")], [full("dg")], v2(T.dg[:], T.idm[:], T.cof[:, 3:4], -1.0 / 64.0, A.mult, A.mult))
    run("p", [full("qk"), full("dg")], [("cn1", 0, 128)], lambda: te.matmul(T.cn1[:, 0:128], T.qk[:], T.dg[:], True, True))
    V([full("idm")], [full("nid")], v1(T.nid[:], T.idm[:], -1.0, A.mult))
    fill("cst2", 0, 128, 63.0 / 128.0)
    V([], [full("cst2")], lambda: v.memset(T.cst2[0:1, :], 255.0))
    c_ts(1)
    c_ts(2)
    V([full("bo"), full("cof")], [full("wto")], v1(T.wto[:], T.bo[:], T.cof[:, 4:5], A.mult))
    V([("cn1", 0, 128)], [full("qm")], vc(T.qm[:], T.cn1[:, 0:128]))
    for i in range(7):
        before(0, i, (0,))
    copy(col("o2f"), col("o2u"))
    claim_rows(0, "o2f", 0, NL)
    weave(claim_list(0))
    S([("pl", 0, WW), full("vl")], [full("v0")], lambda: s.activation(T.v0[:], T.pl[:, 0:WW].indirect(T.vl[:, 0:12]), AF.Identity))
    for i in range(8):
        before(0, i, (1,) if i < 7 else (0, 1))
    weave(scatter(0))
    take("y", "m4", T.mo[:], [full("mo")])
    sums(0)
    for i in range(8):
        rise(i)
        if i < 6:
            plain(i)
    copy(col("mof", 0, 384), col(("mo", NL), 0, 384))
    dma("y", T.yv[:, 0:NL], T.par0[0:128:16, :], [full("par0")], [])
    for i in range(5):
        before(1, i)
    step1("dd", False, "mo", "mo", "o2u", "o2f", ("mo", NL), "mof", ("cof", 1), "q1", "t2u1", [nothing, nothing, lambda: scan(0)], 1)
    shifted(1, "q1")
    lots_of("q1")
    stage("y1", T.tf, [full("tf")])
    send("y1")
    scan(1)
    cl = claim_list(1)
    weave(cl[:4])
    scan(2)
    weigh("wto")
    weave(cl[4:])
    before(1, 5)
    weave(scatter(1), [nothing, nothing] + next_lots("q1", "tnu"))
    before(1, 6)
    before(1, 7)
    sums(1)
    for i in range(8):
        rise(i)
        if i < 6:
            plain(i)
    bound_sums()
    bound_sel()
    weave(pick("o2f", "mof", "b1f", 0), pick("pb1", ("mof", NL), "par12", NL))
    copy(col("b1u"), col("b1f"))
    take("y", "y1", T.yh[:, NL:2 * NL], [])
    for i in range(5):
        before(2, i)
    step1("dd", False, "tnu", "tn", "t2u1", ("q1", ODD, 2), "b1u", "b1f", ("cof", 2), "q2", "t2u2", [nothing, nothing, nothing], 2)
    lots_of("q2")
    stage("y2", T.tf, [full("tf")])
    send("y2")
    bound_sums()
    weave(claim_list(2))
    before(2, 5)
    weave(scatter(2), [nothing, bound_sel] + pick("pb2", "par12", ("par12", NL), 0))
    before(2, 6)
    before(2, 7)
    stage("par", T.par12, [full("par12")], rows=True)
    send("par")
    sums(2)

    def price(i):
        lo, hi = 512 * i, 512 * i + 512
        if i < 7:
            S([("dd", lo, hi)], [("pf", lo, hi)], lambda: s.activation(T.pf[:, lo:hi], T.dd[:, lo:hi], AF.Identity, scale=-1.0, bias=MAGIC + 255.0))
        else:
            V([("dd", lo, hi)], [("pf", lo, hi)], v2(T.pf[:, lo:hi], T.dd[:, lo:hi], -1.0, MAGIC + 255.0, A.mult, A.add))

    def ship(b):
        p, rp = col("pf", BLOCKS[b], BLOCKS[b + 1])
        m = "o%d" % b
        dma("y", T["s_" + m][:], p, [rp], [full("s_" + m)])
        dma("y", T["l_" + m][rank], T.pf[mine, BLOCKS[b]:BLOCKS[b + 1]], [rp], [full("l_" + m)])
        send(m)
    nxt = 0
    for i in range(8):
        rise(i)
        price(i)
        if BLOCKS[nxt + 1] <= 512 * i + 512:
            ship(nxt)
            nxt += 1
    take("s", "y2", T.yh[:, 2 * NL:3 * NL], [])
    take("s", "par", T.yv[:, NL:3 * NL], [])
    for b in range(NB):
        take("s", "o%d" % b, T.yp[:, BLOCKS[b]:BLOCKS[b + 1]], [])
    for sem in sorted(total):
        if seen.get(sem, 0) < total[sem]:
            wait("g", sem, total[sem])
